import numpy as np, ml_dtypes
CORES = [24,25,26,27,28,29,30,31]
N = 8
BF = ml_dtypes.bfloat16
def gentries(a):
    return np.ascontiguousarray(a.reshape(8, 16, -1).transpose(0, 2, 1)).reshape(8, -1)
def gtable(e):
    e = np.asarray(e); return np.ascontiguousarray(e.reshape(8, -1, 16).transpose(0, 2, 1)).reshape(128, -1).astype(np.int32)
W, M, H, SC, TH, CAP, RO = 4096, 512, 8, 8, 72, 128, 3
B = 8
LEV = np.arange(H).reshape(1, 1, H, 1)
def parts(rng):
    weak = rng.random((N, 8, 1, W)) < rng.choice(np.array([0.15, 0.3, 0.5]), (N, 8, 1, 1))
    size = np.where(weak, 0.25, rng.choice(np.array([0.5, 1.0]), (N, 8, 1, W)))
    s = (256 * size * rng.random((N, 8, 16, W))).astype(np.int64); w = rng.integers(0, 256, (N, 8, 16, W))
    c = rng.integers(0, W, (N, 8, H, M)); n = rng.integers(1, H + 1, (N, 8, M)); to = np.argsort(rng.random((N, 8, M)), axis=-1)
    return s, w, c, n, to
def pack(s, w, c, n, to):
    return {"st": s.reshape(N, 128, W).astype(np.float32).astype(BF), "wt": w.reshape(N, 128, W).astype(np.float32).astype(BF),
            "cs": np.stack([gtable(a.reshape(8, -1)) for a in c]), "ns": np.stack([gtable(a) for a in n]), "ds": np.stack([gtable(a) for a in to])}
def plant(rng, s, w, edge):
    k = 17 * B; pc = 1 + np.argsort(rng.random((N, 8, W - 1)), axis=-1)[..., :k]
    yes = (np.argsort(rng.random((N, 8, k, 16)), axis=-1) < np.repeat(np.arange(17), B)[:, None]).transpose(0, 1, 3, 2)
    ix = np.ascontiguousarray(np.broadcast_to(pc[:, :, None, :], (N, 8, 16, k)))
    if edge:
        a = rng.integers(1, 256 // SC, yes.shape); b = SC * a + yes
    else:
        a = np.where(yes, 0, 255); b = rng.integers(1, 256, yes.shape)
    np.put_along_axis(s, ix, a, 3); np.put_along_axis(w, ix, b, 3); s[..., 0] = 255
    return pc
def stacks(rng, pc, j):
    e = np.take_along_axis(pc, (j * B + rng.integers(0, B, j.shape)).reshape(N, 8, H * M), 2).reshape(j.shape)
    return np.where(LEV % 2 == 1, e, 0)
def setup_inputs(rng):
    return pack(*parts(rng))
def setup_inputs_room(rng):
    s, w, c, n, to = parts(rng); pc = plant(rng, s, w, False); n = rng.integers(2, H + 1, (N, 8, M))
    cnt = rng.permuted(np.tile(np.array([M, M // 2, M // 2, CAP + 1, CAP, CAP - 1, 1, 0]), (N, 1)), axis=1)
    pos = np.argsort(rng.random((N, 1, M)), axis=-1)
    top = np.where(pos < cnt[:, :, None], 16, 8)[:, :, None]
    kk = (1 + 2 * (rng.integers(0, H, (N, 8, M)) % (n // 2)))[:, :, None]
    j = np.where(LEV == kk, top, np.minimum(rng.integers(0, 17, (N, 8, H, M)), top))
    return pack(s, w, stacks(rng, pc, j), n, to)
def setup_inputs_ties(rng):
    s, w, c, n, to = parts(rng); pc = plant(rng, s, w, True)
    goal = TH - 1 + rng.integers(0, 3, (N, 1, M)); j = goal // 8 + (np.arange(8)[:, None] < goal % 8)
    e = rng.integers(0, min(15 - (TH + 1) // 8, (TH - 1) // 8) + 1, (N, 4, M))
    j = rng.permuted(np.concatenate([j[:, :4] + e, j[:, 4:] - e], axis=1), axis=1)
    m = np.arange(M); h = M // 2
    n = np.where(m < CAP // 4, rng.integers(4, H + 1, (N, 8, M)), np.where(m < h, 2, n))
    c = np.where(m < h, stacks(rng, pc, np.repeat(j[:, :, None], H, axis=2)), c)
    return pack(s, w, c, n, to)
def setup_inputs_alike(rng):
    s, w, c, n, to = parts(rng); half = rng.random((N, 1, M)) < 0.5
    n = np.where(half, rng.choice(np.array([1, 2, H - 1, H]), (N, 8, M)), n)
    c = np.where(half[:, :, None], rng.choice(np.array([0, 1, W // 2, W - 1]), (N, 8, H, M)), c)
    i = np.arange(M); to[:, 0] = i; to[:, 1] = i[::-1]; to[:, 2] = (i + 1) % M
    w[:, 3] = 255 * rng.integers(0, 2, (N, 16, W))
    return pack(s, w, c, n, to)
def setup_inputs_full(rng):
    s, w, c, n, to = parts(rng)
    n = np.where(rng.random((N, 8, M)) < 0.9, H - rng.integers(0, 2, (N, 8, M)), n)
    q = int(rng.integers(0, N)); a = (q + 1) % N; b = (q + int(rng.integers(2, N))) % N; g = rng.permutation(8)
    n[b, g[0]] = 1; s[q, g[1]] = 255
    n[a, g[1]] = H; c[a, g[1]] -= c[a, g[1]] % 2
    w[a, g[1], :, ::2] = 0; s[a, g[1], :, 1::2] = 0
    x = np.append(rng.permutation(M - 1)[:CAP - 1], M - 1); y = 1 + 2 * rng.integers(0, W // 2, (8, CAP))
    for k in range(8):
        c[a, k, 0, x] = 0; c[a, k, 1, x] = y[k]; n[a, k, x] = np.maximum(n[a, k, x], 2)
        sk = s[a, k]; wk = w[a, k]
        sk[:, y[k]] = 0; wk[:, y[k]] = np.maximum(wk[:, y[k]], 1)
    return pack(s, w, c, n, to)
def setup_inputs_spread(rng):
    s, w, c, n, to = parts(rng)
    s = (np.exp2(8 * rng.random((N, 8, 1, W))) * rng.random((N, 8, 16, W))).astype(np.int64)
    w = (np.exp2(8 * rng.random((N, 8, 1, W))) * rng.random((N, 8, 16, W))).astype(np.int64)
    return pack(s, w, c, n, to)
def check_inputs(d):
    bad = []
    for k in ("st", "wt"):
        a = np.asarray(d[k]).astype(np.float32)
        if not (np.all(a >= 0) and np.all(a <= 255) and np.all(a == np.floor(a))): bad.append("whole numbers of " + k)
    for k, lo, hi in (("cs", 0, W - 1), ("ns", 1, H), ("ds", 0, M - 1)):
        if np.min(d[k]) < lo or np.max(d[k]) > hi: bad.append("range of " + k)
    if np.any(np.sort(np.stack([gentries(a) for a in d["ds"]]), axis=-1) != np.arange(M)): bad.append("targets of a group differ")
    return bad
def reference(st, wt, cs, ns, ds):
    s = st.astype(np.float32).astype(np.int32).reshape(N, 8, 16, W); w = wt.astype(np.float32).astype(np.int32).reshape(N, 8, 16, W)
    c = np.stack([gentries(a) for a in cs]).astype(np.int64).reshape(N, 8, H, M); n = np.stack([gentries(a) for a in ns]).astype(np.int64)
    inv = np.argsort(np.stack([gentries(a) for a in ds]), axis=-1)
    imp = np.zeros((N, 8, 16, M), np.int64); site = np.arange(M)
    for t in range(RO):
        live = LEV < n[:, :, None]; c = np.where(live, c, 0)
        rho = np.take_along_axis(w, c.reshape(N, 8, 1, H * M), 3).reshape(N, 8, 16, H, M) * live[:, :, None]
        own = np.add.accumulate(rho[:, :, :, ::-1], axis=3)[:, :, :, ::-1]
        low = np.concatenate([c[:, :, :1], c[:, :, :-1]], axis=2)
        h = (((c * low) >> 5) + c + 77 * t) & (W - 1)
        over = own + imp[:, :, :, None] > SC * np.take_along_axis(s, h.reshape(N, 8, 1, H * M), 3).reshape(N, 8, 16, H, M)
        v = np.where(live & (LEV > 0), np.add.reduce(over.astype(np.int64), axis=2), 0)
        most = np.max(v, axis=2); ks = np.argmax(v, axis=2)
        c = np.where(live, (13 * c + 97 * v + t) & (W - 1), 0)
        ready = (most >= 9) & (np.add.reduce(most, axis=1, keepdims=True) >= TH); one = ready.astype(np.int64)
        slide = ready & (np.add.accumulate(one, axis=2) - one < CAP)
        load = np.take_along_axis(own, ks[:, :, None, None], 3)[:, :, :, 0]
        old = n; grow = ~slide & (old < H)
        top = np.take_along_axis(c, old[:, :, None] - 1, 2)[:, :, 0]
        e = np.where(grow[:, :, None] & (LEV == old[:, :, None]), ((31 * site + 997 * t + top) & (W - 1))[:, :, None], c)
        n = np.where(slide, ks, old + grow)
        nc, nn, ni = [], [], []
        for a in range(N):
            q = (a - 1 - t % (N - 1)) % N; i = inv[q]
            got = np.take_along_axis(slide[q], i, 1); k0 = np.take_along_axis(ks[q], i, 1); end = np.take_along_axis(old[q], i, 1)
            row = LEV[0] - n[a][:, None] + k0[:, None]
            run = np.take_along_axis(np.take_along_axis(c[q], i[:, None], 2), np.clip(row, 0, H - 1), 1)
            hit = got[:, None] & (row >= k0[:, None]) & (row < end[:, None])
            nc.append(np.where(hit, run, e[a])); nn.append(np.minimum(n[a] + got * (end - k0), H))
            ni.append(np.take_along_axis(load[q], i[:, None], 2) * got[:, None])
        c = np.stack(nc); n = np.stack(nn); imp = np.stack(ni)
    c = np.where(LEV < n[:, :, None], c, -1)
    return {"yc": np.stack([gtable(a.reshape(8, -1)) for a in c]).astype(np.float32), "yn": np.stack([gtable(a) for a in n]).astype(np.float32), "yi": imp.reshape(N, 128, M).astype(np.float32)}

@@ -1,0 +1,542 @@
+from concourse.mybir import AluOpType as A, ActivationFunctionType as F
+
+RO = 3
+TOPS = ((4,), (7, 3))
+ORDER = ("K S s6 o7 o6 s7 I P t6 s3 s4 o5 t7 t3 o4 c6 o3 s2 c7 o2 u4 c3 t4 t2 s5 c2 s1 o1 c4 n3 t5 c5 n2 t1 c1 n4 n1 H",
+         "S P s4 t4 s5 o7 s6 o6 o5 u7 t5 s7 s3 o4 t7 c7 s2 c4 s1 o3 c5 t6 t3 n4 o2 u3 t2 c6 t1 c3 K c2 n3 c1 n2 n1 H")
+BANKS = ({6: 1, 7: 2, 3: 3, 4: 5, 2: 1, 5: 2, 1: 3}, {4: 1, 7: 2, 5: 3, 6: 5, 3: 1, 2: 2, 1: 3})
+SCANS = ((1, 0), (2, 0), (3, 0), (4, 0), (1, 1), (2, 1), (5, 0), (3, 1), (4, 1), (6, 0), (5, 1), (7, 0), (6, 1), (7, 1))
+DEAD = 65536.0
+SW2 = 8368
+SD2 = 8352
+
+f32, bf, i32, u16 = "float32", "bfloat16", "int32", "uint16"
+
+
+def sb(dt, *shape):
+    return ("sbuf", [128] + list(shape), dt)
+
+
+SCRATCH = {
+    "W": sb(bf, 4112), "S0": sb(bf, 4112), "S2": sb(bf, SW2), "csI": sb(i32, 256), "nsI": sb(i32, 32), "dsI": sb(i32, 32),
+    "SG": sb(bf, 3584), "OV1": sb(bf, 64, 16), "OV2": sb(bf, 64, 16), "OV3": sb(bf, 64, 16), "OV4": sb(bf, 32, 16),
+    "LD": sb(f32, 512), "YI": sb(f32, 512), "IM": sb(f32, 512), "RH": sb(bf, 512),
+    "C13": sb(f32, 256), "MX": sb(f32, 256), "XI": sb(i32, 256), "CP": sb(i32, 256),
+    "PB": sb(bf, 544), "FW": sb(bf, 1056), "RT": sb(bf, 16, 32), "SO": sb(f32, 1792),
+    "D0": sb(bf, 256), "D1": sb(bf, 256), "GA": sb(bf, 256), "GT": sb(bf, 1792),
+    "PR": sb(i32, 224), "QI": sb(i32, 224), "HI": sb(i32, 224), "cW": sb(u16, 224), "hS": sb(u16, 224),
+    "GP": sb(f32, 224), "EI": sb(i32, 256), "EA": sb(i32, 256), "YY": sb(f32, 256), "ZZ": sb(f32, 256), "SC": sb(f32, 256),
+    "sm": sb(f32, 16 * 32), "smi": sb(i32, 4 * 32), "OF": sb(u16, 32), "RD": sb(bf, 32), "CS": sb(bf, 48), "ONE": sb(bf, 32),
+    "I8": sb(bf, 128), "NI": sb(f32, 128), "NB": sb(bf, 128), "Z1": sb(f32, 144), "ZA": sb(bf, 144), "ZB": sb(bf, 144),
+    "Z16": sb(f32, 144), "GB": sb(bf, 128), "TRI": sb(bf, 128), "SR": sb(f32, 128), "SH": sb(f32, 160), "SHM": sb(bf, 4 * 160),
+    "NKC": sb(f32, 512), "RM": sb(f32, 256), "DPC": sb(bf, 136), "PC": sb(bf, 32),
+    "GI": sb(f32, 256), "GD": sb(f32, 3 * 256), "SI": sb(f32, 512), "SV": sb(f32, 512),
+    "pI": sb(i32, 8), "col": sb(f32, 16), "IO": sb(f32, 128),
+    "K2S": sb(u16, 16), "S2K": sb(u16, 16), "dsU": sb(u16, 32), "invL": sb(u16, 32), "invP": sb(u16, 32),
+}
+for _b in range(8):
+    SCRATCH["B%d" % _b] = ("psum", [128, 512], f32)
+for _t in range(RO):
+    SCRATCH["OWN%d" % _t] = sb(f32, 4096)
+    SCRATCH["GS%d" % _t] = sb(bf, 512)
+    SCRATCH["RX%d" % _t] = sb(bf, 16, 32)
+    SCRATCH["LP%d" % _t] = sb(f32, 512)
+for _t in range(RO + 1):
+    SCRATCH["C%d" % _t] = sb(f32, 256)
+
+SEMAPHORES = (["cV", "cA", "cP", "cG"] + ["d%d" % k for k in range(12)]
+              + [n + str(t) for n in ("arrP", "arrL", "sntP", "sntL") for t in range(RO)])
+
+
+def emit(ops, g, T):
+    queue = {"V": g.vector, "A": g.scalar, "P": g.tensor, "G": g, "Y": g.sync}
+    known = {q: {} for q in queue}
+    lastw, readers, bank, count = {}, {}, {}, {}
+    waits, snap, ident, needed = [], [], [], set()
+    for j, op in enumerate(ops):
+        q = op["q"]
+        deps = set()
+        for tk in op["r"]:
+            if tk in lastw:
+                deps.add(lastw[tk])
+        for tk in op["w"]:
+            if tk in lastw:
+                deps.add(lastw[tk])
+            deps.update(readers.get(tk, []))
+        banks = set(tk[:2] for tk in op["r"] + op["w"] if tk[0] == "B" and tk[1].isdigit())
+        for b in banks:
+            for oq, d in bank.get(b, {}).items():
+                if oq != q:
+                    deps.add(d)
+        wl = []
+        for d in sorted(deps, reverse=True):
+            key, seq = ident[d]
+            if key == "P" and q == "P":
+                continue
+            if known[q].get(key, -1) >= seq:
+                continue
+            wl.append(d)
+            needed.add(d)
+            for k2, s2 in snap[d].items():
+                if known[q].get(k2, -1) < s2:
+                    known[q][k2] = s2
+        waits.append(wl)
+        if op["sem"] is None:
+            key = q
+            seq = count.get(q, 0)
+            count[q] = seq + 1
+        else:
+            key, seq = op["sem"], 0
+        ident.append((key, seq))
+        s = {} if op["ext"] else dict(known[q])
+        s[key] = seq
+        snap.append(s)
+        if op["fn"] is not None or op["ext"]:
+            for tk in op["r"]:
+                readers.setdefault(tk, []).append(j)
+        for tk in op["w"]:
+            lastw[tk] = j
+            readers[tk] = []
+        for b in banks:
+            bank.setdefault(b, {})[q] = j
+    value, run = {}, {}
+    for j, op in enumerate(ops):
+        if op["sem"] is not None:
+            value[j] = (op["sem"], op["n"])
+        elif j in needed:
+            run[op["q"]] = run.get(op["q"], 0) + 1
+            value[j] = ("c" + op["q"], run[op["q"]])
+    for j, op in enumerate(ops):
+        for d in waits[j]:
+            queue[op["q"]].wait_ge(T.sem[value[d][0]], value[d][1])
+        if op["fn"] is None:
+            continue
+        ins = op["fn"]()
+        if op["own"]:
+            continue
+        if op["sem"] is not None:
+            ins.then_inc(T.sem[op["sem"]], op["n"])
+        elif j in needed:
+            ins.then_inc(T.sem["c" + op["q"]], 1)
+
+
+def rank_program(g, core, T, topo):
+    rank = T.rank_of(core)
+    if rank is None:
+        return
+    N = len(T.cores)
+    ops = []
+    V, S, P = g.vector, g.scalar, g.tensor
+
+    def add(q, fn, r, w, sem=None, n=0, ext=False, own=False):
+        ops.append({"q": q, "fn": fn, "r": list(r), "w": list(w), "sem": sem, "n": n, "ext": ext, "own": own})
+
+    def tt(out, a, b, op, r, w):
+        add("V", lambda: V.tensor_tensor(out, a, b, op), r, w)
+
+    def ts(out, a, s1, op0, r, w, s2=None, op1=None):
+        if op1 is None:
+            add("V", lambda: V.tensor_scalar(out, a, s1, None, op0), r, w)
+        else:
+            add("V", lambda: V.tensor_scalar(out, a, s1, s2, op0, op1), r, w)
+
+    def cp(out, a, r, w):
+        add("V", lambda: V.tensor_copy(out, a), r, w)
+
+    def ms(ap, v, w):
+        add("V", lambda: V.memset(ap, v), [], w)
+
+    def scan(out, d0, d1, op0, op1, r, w):
+        add("V", lambda: V.tensor_tensor_scan(out, d0, d1, 0.0, op0, op1), r, w)
+
+    def tr(out, a, r, w):
+        add("V", lambda: V.transpose(out, a), r, w)
+
+    def act(out, a, fn, r, w, bias=0.0, scale=1.0):
+        add("A", lambda: S.activation(out, a, fn, bias=bias, scale=scale), r, w)
+
+    def mm(out, lhsT, rhs, start, stop, r, w):
+        add("P", lambda: P.matmul(out, lhsT, rhs, start, stop), r, w)
+
+    def iota(out, pat, base, cm, w, isint=False):
+        if isint:
+            add("G", lambda: g.iota(out, pat, base, cm), [], w)
+        else:
+            add("G", lambda: g.iota(out, pat, base, cm, allow_small_or_imprecise_dtypes=True), [], w)
+
+    def fill(out, n, v, w):
+        iota(out, [[0, n]], v, 0, w)
+
+    def sel(out, a, pat, op, fv, base, cm, r, w):
+        add("G", lambda: g.affine_select(out, a, pat, op, fv, base, cm), r, w)
+
+    nd = [0]
+
+    def dma(q, out, a, r, w):
+        e = g.sync if q == "Y" else g.scalar
+        add(q, lambda: e.dma_start(out, a), r, w, sem="d%d" % nd[0], n=16)
+        nd[0] += 1
+
+    def send(dst, out, src, e, arr, snt, toks):
+        rid, pid = topo.addr(dst)[:2]
+        m = sum(1 << k for k in e)
+        add("G", lambda: g.remote_dma(out, src, T.sem[arr], T.sem[snt], pid, rid, m), toks, [snt], sem=snt, n=len(e), own=True)
+
+    def sm(k):
+        return T.sm[:, 32 * k:32 * k + 32]
+
+    def smi(k):
+        return T.smi[:, 32 * k:32 * k + 32]
+
+    def col(k):
+        return T.col[:, k:k + 1]
+
+    (THR, NM, G1, M15, NP, W5, OFF, NPM, RL, BB, S4096, YV, ZV, C873) = range(14)
+    (cR, cGam, cK2S, c8R, c31, c31b, c31c, cNR, cB0, cB1, cC0, cC1, cT0, cT1) = range(14)
+    ZT = ["ZZ%d" % k for k in range(8)]
+
+    dma("A", T.dsI[:], T.ds[:], [], ["dsI"])
+    dma("A", T.nsI[:], T.ns[:], [], ["nsI"])
+    dma("A", T.csI[:], T.cs[:], [], ["csI"])
+    dma("Y", T.W[:, 0:4096], T.wt[:], [], ["Wa"])
+    dma("Y", T.S0[:, 0:4096], T.st[:], [], ["S0a"])
+    add("Y", None, ["S0a"], [])
+    dma("Y", T.S2[:, 0:4096], T.st[:], [], ["S2a"])
+    dma("Y", T.S2[:, 4096:8192], T.st[:], [], ["S2b"])
+    dma("Y", T.S2[:, 8192:SD2], T.st[:, 0:160], [], ["S2c"])
+
+    def key_const(v):
+        iota(T.NKC[:, 256 * v:256 * v + 256], [[0, 32], [1, 8]], -16, 0, ["NKC%d" % v])
+        for k in TOPS[v]:
+            fill(T.NKC[:, 256 * v + k:256 * v + 256:8], 32, k - 16 - 12416, ["NKC%d" % v])
+
+    iota(T.pI[:, 0:1], [[0, 1]], 0, 1, ["pI0"], True)
+    iota(T.SI[:], [[1, 512]], 64, 0, ["SI"])
+    iota(T.IO[:, 16:32], [[2, 16]], 0, 0, ["IOb"])
+    key_const(0)
+    z8 = T.Z1[:, 15:128:16]
+    ms(T.Z1[:], 0.0, ["Z1"])
+    ms(T.I8[:], 8.0, ["I8"])
+    ms(T.NI[:], -1.0, ["NI"])
+    ms(z8, 1.0, ["Z1"])
+    ms(T.GB[:], -16.0, ["GB"])
+    ms(T.SH[:], 1.0, ["SH"])
+    sel(T.I8[:], T.I8[:], [[-1, 128]], A.is_equal, 0.0, 0, 1, ["I8"], ["I8"])
+    sel(T.NI[:], T.NI[:], [[-1, 128]], A.is_equal, 0.0, 0, 1, ["NI"], ["NI"])
+    sel(z8, z8, [[-16, 8]], A.is_ge, 0.0, 0, 1, ["Z1"], ["Z1"])
+    iota(T.SR[:], [[0, 8], [1, 16]], 0, 0, ["SR"])
+    sel(z8, z8, [[16, 8]], A.is_ge, 0.0, 15, -1, ["Z1"], ["Z1"])
+    iota(T.IO[:, 64:96], [[16, 32]], 0, 0, ["IOd"])
+    iota(T.IO[:, 32:48], [[1, 8], [128, 2]], 0, 0, ["IOc"])
+    sel(T.GB[:], T.GB[:], [[-16, 8], [0, 16]], A.is_ge, 0.0, 0, 1, ["GB"], ["GB"])
+    sel(T.SH[:], T.SH[:], [[1, 160]], A.is_equal, 0.0, -16, -1, ["SH"], ["SH"])
+    sel(T.GB[:], T.GB[:], [[16, 8], [0, 16]], A.is_ge, 0.0, 15, -1, ["GB"], ["GB"])
+    iota(T.GI[:], [[496, 32], [0, 8]], 4096, 0, ["GI"])
+    sel(T.TRI[:], T.GB[:], [[1, 128]], A.is_gt, 0.0, 0, -1, ["GB"], ["TRI"])
+    fill(T.RM[:], 256, 1, ["RM"])
+    sel(T.TRI[:], T.TRI[:], [[1, 128]], A.not_equal, 16384.0, 0, -1, ["TRI"], ["TRI"])
+    fill(T.RM[:, 0:256:8], 32, 0, ["RM"])
+    fill(T.PB[:], 544, 0, ["PBh", "PBl", "PB14", "PB15"])
+    fill(T.DPC[:], 136, 0, ["DPC"])
+    fill(T.D0[:], 256, 1, ["D0"])
+    fill(T.DPC[:, 14:136:8], 16, -16384, ["DPC"])
+    fill(T.D1[:], 256, 1048576, ["D1"])
+    fill(T.DPC[:, 15:136:8], 16, 16384, ["DPC"])
+    fill(T.D0[:, 0:256:8], 32, 1048576, ["D0"])
+    key_const(1)
+
+    ms(T.W[:, 4096:4112], 0.0, ["Wb"])
+    ms(T.S0[:, 4096:4112], 1024.0, ["S0b"])
+    ms(T.S2[:, SD2:SW2], 1024.0, ["S2d"])
+    ms(T.OWN0[:, 0:512], 0.0, ["OWN0.0"])
+    ms(T.ONE[:], 1.0, ["ONE"])
+    ms(T.CS[:], 0.0, ["CS"])
+    ms(T.PC[:], -1792.0, ["PC"])
+    ms(sm(C873), 873.0, ["C873"])
+    ts(T.pI[:, 1:2], T.pI[:, 0:1], 15, A.bitwise_and, ["pI0"], ["pI1"])
+    ts(T.pI[:, 2:3], T.pI[:, 0:1], 4, A.logical_shift_right, ["pI0"], ["pI2"], 1, A.bitwise_and)
+    ts(T.pI[:, 3:4], T.pI[:, 0:1], 7, A.bitwise_and, ["pI0"], ["pI3"])
+    ts(T.pI[:, 4:5], T.pI[:, 0:1], 3, A.logical_shift_right, ["pI0"], ["pI4"], 1, A.bitwise_and)
+    cp(col(cR), T.pI[:, 1:2], ["pI1"], ["cR"])
+    ts(col(cT0), T.pI[:, 3:4], 32.0, A.mult, ["pI3"], ["cT0"])
+    cp(col(cGam), T.pI[:, 2:3], ["pI2"], ["cGam"])
+    cp(T.dsU[:], T.dsI[:], ["dsI"], ["dsU"])
+    add("A", lambda: S.activation(T.SV[:, 0:512].indirect(T.dsU[:, 0:32]), T.SI[:], F.Silu), ["dsU", "SI"], ["SV"])
+    tt(col(cK2S), col(cT0), T.pI[:, 4:5], A.add, ["cT0", "pI4"], ["cK2S"])
+
+    def act_consts():
+        act(T.Z16[:], T.Z1[:], F.Identity, ["Z1"], ["Z16"], scale=0.0625)
+        act(T.ZA[:], T.Z1[:], F.Identity, ["Z1"], ["ZA"], scale=1552.0)
+        act(T.ZB[:], T.Z1[:], F.Identity, ["Z1"], ["ZB"], scale=776.0)
+        act(T.NB[:], T.NI[:], F.Identity, ["NI"], ["NB"])
+        act(col(c8R), col(cR), F.Identity, ["cR"], ["c8R"], scale=8.0)
+        for t in range(RO):
+            act(col(c31 + t), col(cR), F.Identity, ["cR"], ["c31%d" % t], scale=31.0, bias=997.0 * t)
+        act(col(cNR), col(cR), F.Identity, ["cR"], ["cNR"], scale=-1.0)
+        act(col(cB0), col(cGam), F.Identity, ["cGam"], ["cB0"], scale=-400.0, bias=-100.0)
+        act(col(cB1), col(cGam), F.Identity, ["cGam"], ["cB1"], scale=400.0, bias=-500.0)
+        act(col(cC0), col(cGam), F.Identity, ["cGam"], ["cC0"], scale=528.0, bias=-64.0)
+        act(col(cC1), col(cGam), F.Identity, ["cGam"], ["cC1"], scale=-1056.0, bias=528.0)
+        act(col(cT1), col(cR), F.Identity, ["cR"], ["cT1"], bias=4096.0)
+        act(T.SR[:], T.SR[:], F.Abs, ["SR", "cNR"], ["SR"], bias=col(cNR))
+        act(sm(S4096), T.IO[:, 64:96], F.Identity, ["IOd", "cT1"], ["S4096"], bias=col(cT1))
+        act(T.SR[:], T.SR[:], F.Relu, ["SR"], ["SR"], scale=-1.0 / 128, bias=1.0 / 128)
+
+    def act_consts_late():
+        for k, nm in enumerate(("cB0", "cB1")):
+            act(T.SHM[:, 160 * k:160 * k + 160], T.SH[:], F.Sigmoid, ["SH", nm], ["SHM%d" % k], scale=200.0, bias=col(cB0 + k))
+        act(T.SHM[:, 320:640], T.SHM[:, 0:320], F.Identity, ["SHM0", "SHM1"], ["SHM2", "SHM3"], scale=-1.0)
+
+    def grow_const(t):
+        act(T.GD[:, 256 * t:256 * t + 256], T.GI[:], F.Identity, ["GI", "c31%d" % t], ["GD%d" % t], bias=col(c31 + t))
+
+    def shm(beta, gam, neg):
+        a = 160 * (beta + 2 * neg) + 16 - 16 * (gam - beta)
+        return T.SHM[:, a:a + 128]
+    SHT = ["SHM%d" % k for k in range(4)] + ["RT"]
+
+    def levels(out, sign, w):
+        for k in range(1, 8):
+            act(out[:, 32 * k:32 * k + 32], sm(NP), F.Identity, ["NP"], [w % k], scale=-2 * DEAD * sign,
+                bias=sign * DEAD * (2 * k + 1))
+
+    def invert_p():
+        for r in range(16):
+            mm(T.B7[:, 224:256], T.Z16[:, 15 - r:143 - r], T.SV[:, r:512:16], r == 0, r == 15, ["Z16", "SV"], ["B7i"])
+
+    def invert_b():
+        cp(smi(1), T.B7[:, 224:256], ["B7i"], ["si"])
+        ts(T.S2K[:], T.IO[:, 32:48], col(c8R), A.add, ["IOc", "c8R"], ["S2K"])
+        ts(smi(2), smi(1), 4, A.logical_shift_right, ["si"], ["par"], 1, A.bitwise_and)
+        ts(T.invL[:], smi(1), -64.0, A.add, ["si"], ["invL"])
+        ts(sm(YV), smi(2), col(cC1), A.mult, ["par", "cC0", "cC1"], ["YV"], col(cC0), A.add)
+        tt(sm(ZV), sm(YV), smi(1), A.add, ["YV", "si"], ["ZV"])
+        cp(T.invP[:, 0:32:2], T.sm[:, 32 * ZV:32 * ZV + 16], ["ZV"], ["invPa"])
+        cp(T.invP[:, 1:32:2], T.sm[:, 32 * ZV + 16:32 * ZV + 32], ["ZV"], ["invPb"])
+
+    for k in range(8):
+        ts(T.ZZ[:, 32 * k:32 * k + 32], T.nsI[:], -2 * DEAD, A.mult, ["nsI"], ["ZZ%d" % k], DEAD * (2 * k + 1), A.add)
+    ts(sm(NM), T.nsI[:], -16.0, A.add, ["nsI"], ["NM"])
+    tt(T.YY[:], T.ZZ[:], T.csI[:], A.max, ZT + ["csI"], ["YY"])
+    ts(sm(G1), T.nsI[:], 1.0, A.add, ["nsI"], ["G1"], 8.0, A.min)
+    ts(T.C0[:], T.YY[:], DEAD, A.min, ["YY"], ["C0"])
+    ts(T.K2S[:], T.IO[:, 16:32], col(cK2S), A.add, ["IOb", "cK2S"], ["K2S"])
+
+    for t in range(RO):
+        C, Cn, OWN = T["C%d" % t], T["C%d" % (t + 1)], T["OWN%d" % t]
+        c, cn = "C%d" % t, "C%d" % (t + 1)
+        last = t == RO - 1
+        ver = min(t, 1)
+        TOP, tb, order = TOPS[ver], BANKS[ver], ORDER[ver].split()
+        fin = int([x for x in order if x[0] == "n"][-1][1])
+
+        def ow(b):
+            return "OWN%d.%d" % (t, b)
+
+        ts(T.cW[:], C[:, 32:256], 4096.0, A.min, [c], ["cW"])
+        ts(T.B6[:, 0:224], C[:, 0:224], 4096.0, A.min, [c, c + "a"], ["B6a"])
+        if t > 0:
+            act(T.B7[:, 0:224], C[:, 32:256], F.Identity, [c], ["B7a"], bias=77.0 * t)
+            act(T.RH[:], T.W[:, 0:4112].indirect(T.cW[:, 0:32]), F.Identity, ["Wa", "Wb", "cW"], ["RH"])
+        tt(T.PR[:], C[:, 32:256], T.B6[:, 0:224], A.mult, [c, "B6a"], ["PR"])
+        ts(T.QI[:], T.PR[:], 5, A.logical_shift_right, ["PR"], ["QI"], 4095, A.bitwise_and)
+        if t == 0:
+            tt(T.HI[:], T.QI[:], C[:, 32:256], A.add, ["QI", c], ["HI"])
+            ts(T.QI[:], T.HI[:], 0x10FFF, A.bitwise_and, ["HI"], ["QI"])
+            ts(T.hS[:], T.QI[:], 4096.0, A.min, ["QI"], ["hS"])
+            win, wtok = T.S0[:, 0:4112], ["S0a", "S0b"]
+            act_consts()
+        else:
+            tt(T.HI[:], T.QI[:], T.B7[:, 0:224], A.add, ["QI", "B7a"], ["HI"])
+            ts(T.hS[:], T.HI[:], float(SD2), A.min, ["HI"], ["hS"])
+            win, wtok = T.S2[:, 0:SW2], ["S2a", "S2b", "S2c", "S2d"]
+        mm(T.B0[:, 0:256], T.NI[:], T.NKC[:, 256 * ver:256 * ver + 256], True, False, ["NI", "NKC%d" % ver], ["B0k"])
+
+        begun = set()
+
+        def o(k):
+            b = 8 - k
+            tt(OWN[:, 512 * b:512 * b + 512], T.W[:, 0:4112].indirect(T.cW[:, 32 * k - 32:32 * k]),
+               OWN[:, 512 * b - 512:512 * b], A.add, ["Wa", "Wb", "cW", ow(b - 1)], [ow(b)])
+
+        def sg(k):
+            act(T.SG[:, 512 * k - 512:512 * k], win.indirect(T.hS[:, 32 * k - 32:32 * k]), F.Identity,
+                wtok + ["hS"], ["SG%d" % k])
+
+        def tm(k):
+            b = tb[k]
+            apart = k == 1 and t > 0
+            mm(T["B%d" % b][:], T.I8[:], T.SG[:, 512 * k - 512:512 * k], k not in begun,
+               (k in begun or k not in TOP) and not apart, ["I8", "SG%d" % k], ["B%dt" % b])
+            if apart:
+                mm(T["B%d" % b][:], T.NB[:], T.RH[:], False, True, ["NB", "RH"], ["B%dt" % b])
+            begun.add(k)
+
+        def to(k):
+            b = tb[k]
+            mm(T["B%d" % b][:], T.NI[:], OWN[:, 512 * (8 - k):512 * (9 - k)], k not in begun, k in begun,
+               ["NI", ow(8 - k)], ["B%dt" % b])
+            begun.add(k)
+
+        def cmp(k):
+            b = tb[k]
+            out = T.OV4[:] if k == 4 else T["OV%d" % (k % 4)][:, k // 4:64:2, :]
+            if k in TOP:
+                act(out, T["B%d" % b][:], F.Sign, ["B%dt" % b], ["OV%d" % k], scale=-1.0, bias=-0.5)
+            else:
+                x = 6 if k == 1 and t > 0 else 8 - k
+                tt(out, OWN[:, 512 * x:512 * x + 512], T["B%d" % b][:], A.is_gt, [ow(x), "B%dt" % b], ["OV%d" % k])
+
+        def cnt(k):
+            z, zt = (T.ZB, "ZB") if k in TOP else (T.ZA, "ZA")
+            for r in range(16):
+                if k == 4:
+                    mm(T.B0[:, 4:256:8], z[:, 15 - r:143 - r], T.OV4[:, :, r], False, k == fin and r == 15, [zt, "OV4"], ["B0k"])
+                else:
+                    mm(T.B0[:, k:256:4], z[:, 15 - r:143 - r], T["OV%d" % k][:, :, r], False, k == fin and r == 15,
+                       [zt, "OV%d" % k, "OV%d" % (k + 4)], ["B0k"])
+
+        def heights():
+            if t > 0:
+                tt(sm(BB), sm(RL), sm(NP), A.add, ["RL", "NP"], ["BB"])
+                ts(sm(NM), sm(BB), 8.0, A.min, ["BB"], ["NM"], -16.0, A.add)
+                ts(sm(G1), sm(BB), 1.0, A.add, ["BB"], ["G1"], 8.0, A.min)
+            else:
+                invert_b()
+
+        def sum_const():
+            mm(T.B4[:, 256:288], T.NI[:], sm(C873), True, False, ["NI", "C873"], ["B4s"])
+
+        def pre_const():
+            mm(T.B7[:, 256:288], T.I8[:], T.PC[:], True, False, ["I8", "PC"], ["B7p"])
+
+        def keep():
+            act(T.C13[:], C[:, 0:256].indirect(T.K2S[:, 0:16]), F.Identity, [c, c + "a", "K2S"], ["C13"], scale=208.0,
+                bias=16.0 * t - 1.0)
+            if t > 0:
+                act(T.IM[:], OWN[:, 0:512], F.Identity, [ow(0)], ["IM"])
+
+        steps = {"o": o, "s": sg, "t": tm, "u": to, "c": cmp, "n": cnt}
+        for x in order:
+            if x[0] in steps:
+                steps[x[0]](int(x[1]))
+            else:
+                {"I": invert_p, "S": sum_const, "P": pre_const, "H": heights, "K": keep}[x]()
+        if t == 0:
+            act_consts_late()
+
+        mx = T.MX[:, 7:256:8]
+        scan(T.MX[:], T.RM[:], T.B0[:, 0:256], A.mult, A.max, ["RM", "B0k"], ["MX"])
+        mm(T.B4[:, 256:288], T.SR[:], mx, False, True, ["SR", "MX"], ["B4s"])
+        act(sm(THR), mx, F.Relu, ["MX"], ["THR"], scale=-1.0, bias=13968.0)
+        grow_const(t)
+        tt(T.XI[:], T.B0[:, 0:256], T.C13[:], A.add, ["B0k", "C13"], ["XI"])
+        tt(T.RD[:], T.B4[:, 256:288], sm(THR), A.is_ge, ["B4s", "THR"], ["RD"])
+        ts(T.CP[:], T.XI[:], 4, A.logical_shift_right, ["XI"], ["CP"], 0x10FFF, A.bitwise_and)
+        scan(T.CS[:, 1:33], T.ONE[:], T.RD[:], A.mult, A.add, ["ONE", "RD"], ["CS"])
+        mm(T.B7[:, 256:288], T.TRI[:], T.RD[:], False, False, ["TRI", "RD"], ["B7p"])
+        mm(T.B7[:, 256:288], T.GB[:], T.CS[:, 0:32], False, True, ["GB", "CS"], ["B7p"])
+        half = ((T.B4, "B4d"), (T.B3, "B3t"))
+        for bk, tok in half:
+            mm(bk[:, 0:136], T.I8[:], T.DPC[:], True, False, ["I8", "DPC"], [tok])
+        if t > 0:
+            mm(T.B1[:], T.NI[:], OWN[:, 3072:3584], True, False, ["NI", ow(6)], ["B1t"])
+            mm(T.B1[:], T.NB[:], T.RH[:], False, True, ["NB", "RH"], ["B1t"])
+        cp(T.B6[:, 256:512], T.CP[:], ["CP"], ["B6b"])
+        act(T.PB[:, 14:526:2], T.B6[:, 256:512], F.Identity, ["B6b"], ["PBh", "PB14"])
+        cp(smi(0), mx, ["MX"], ["mi"])
+        ts(smi(3), smi(0), 15, A.bitwise_and, ["mi"], ["A15"])
+        tt(T.PB[:, 15:527:2], T.B6[:, 256:512], T.PB[:, 14:526:2], A.subtract, ["B6b", "PBh", "PB14"], ["PBl", "PB15"])
+        act(T.PB[:, 30:528:16], sm(NM), F.Identity, ["NM"], ["PB14"])
+        f15 = T.PB[:, 31:528:16]
+        tt(f15, T.B7[:, 256:288], smi(3), A.min, ["B7p", "A15"], ["PB15"])
+        pb = ["PBh", "PBl", "PB14", "PB15"]
+        tr(T.FW[:, 0:512], T.PB[:, 16:528], pb, ["FWa"])
+        tr(T.FW[:, 512:1056], T.PB[:, 0:544], pb, ["FWb"])
+
+        dst = T.cores[(rank + 1 + t % (N - 1)) % N]
+        eng = topo.engines(core, dst)
+        eP, eL = (eng[0::2], eng[1::2]) if t == 0 else (eng, eng)
+        GS, RX, LP = T["GS%d" % t], T["RX%d" % t], T["LP%d" % t]
+        fw = ["FWa", "FWb", "invPa", "invPb"]
+        act(GS[:, 0:256], T.FW[:, 0:1056].indirect(T.invP[:, 0:16]), F.Identity, fw, ["GSa%d" % t])
+        if t > 0:
+            act(OWN[:, 3584:4096], T.B1[:], F.Identity, ["B1t"], [ow(7)], scale=-1.0)
+        cp(GS[:, 256:512], T.FW[:, 0:1056].indirect(T.invP[:, 16:32]), fw, ["GSb%d" % t])
+        send(dst, RX[:], GS[:], eP, "arrP%d" % t, "sntP%d" % t, ["GSa%d" % t, "GSb%d" % t])
+        ts(sm(M15), f15, -1.0, A.mult, ["PB15"], ["M15"], 16.0, A.add)
+        ts(sm(W5), sm(M15), 8.0, A.min, ["M15"], ["W5"], -512.0, A.mult)
+        tt(sm(NP), sm(M15), sm(G1), A.min, ["M15", "G1"], ["NP"])
+        tt(sm(OFF), sm(W5), sm(S4096), A.add, ["W5", "S4096"], ["OFF"])
+        levels(T.ZZ, 1, "ZZ%d")
+        cp(T.OF[:], sm(OFF), ["OFF"], ["OF"])
+        ownw, owt = OWN[:, 0:4096].indirect(T.OF[:, 0:32]), ["OF"] + [ow(b) for b in range(8)]
+        if t == 0:
+            cp(T.LD[:], ownw, owt, ["LD"])
+        else:
+            tt(T.LD[:], ownw, T.IM[:], A.subtract, owt + ["IM"], ["LD"])
+        act(sm(NPM), sm(NP), F.Identity, ["NP"], ["NPM"], bias=-15.0)
+        if not last:
+            levels(T.B7, -1, "B7z%d")
+        act(LP[:], T.LD[:, 0:512].indirect(T.invL[:, 0:32]), F.Identity, ["LD", "invL"], ["LP%d" % t])
+        if last:
+            levels(T.B7, -1, "B7z%d")
+        zn = ["B7z%d" % k for k in range(1, 8)]
+        send(dst, T.YI[:] if last else T["OWN%d" % (t + 1)][:, 0:512], LP[:], eL, "arrL%d" % t, "sntL%d" % t, ["LP%d" % t])
+        add("G", None, [], ["RX%d" % t], sem="arrP%d" % t, n=len(eP), ext=True)
+        add("G", None, [], ["YI" if last else "OWN%d.0" % (t + 1)], sem="arrL%d" % t, n=len(eL), ext=True)
+
+        scan(T.SC[:], T.GD[:, 256 * t:256 * t + 256], T.B6[:, 256:512], A.add, A.min, ["GD%d" % t, "B6b"], ["SC"])
+        tt(T.EI[:], T.SC[:, 0:256].indirect(T.S2K[:, 0:16]), T.ZZ[:], A.max, ["SC", "S2K"] + ZT, ["EI"])
+        ts(T.EA[:], T.EI[:], 0x10FFF, A.bitwise_and, ["EI"], ["EA"])
+
+        tr(T.RT[:], RX[:], ["RX%d" % t], ["RT"])
+        cp(Cn[:, 0:32], T.EA[:, 0:32], ["EA"], [cn + "a"])
+        if last:
+            tt(T.YY[:, 32:256], T.EA[:, 32:256], T.B7[:, 32:256], A.min, ["EA"] + zn, ["YY"])
+        for beta in range(2):
+            for gam in range(2):
+                mm(T.B5[:, 16 * beta:16 * beta + 16], shm(beta, gam, 0), T.RT[:, :, 16 * gam + 15], gam == 0, gam == 1, SHT, ["B5t"])
+        for beta, (bk, tok) in enumerate(half):
+            for gam in range(2):
+                for h in range(2):
+                    a = 16 * gam + h
+                    mm(bk[:, 8:136], shm(beta, gam, 0), T.RT[:, :, a:16 * gam + 16:2], False, False, SHT, [tok])
+                    mm(bk[:, 7:135], shm(beta, gam, 1), T.RT[:, :, a:16 * gam + 16:2], False, False, SHT, [tok])
+                    mm(bk[:, 7:135:8], shm(beta, gam, 0), T.RT[:, :, a], False, gam == 1 and h == 1, SHT, [tok])
+        for beta in range(2):
+            for x in range(4):
+                gam, fld = x // 2, 14 + x % 2
+                mm(T.B1[:, 16 * beta:16 * beta + 16], shm(beta, gam, 0), T.RT[:, :, 16 * gam + fld], x == 0, x == 3, SHT, ["B1t"])
+        tt(T.D1[:, 0:256:8], T.B5[:, 0:32], sm(NPM), A.add, ["B5t", "NPM"], ["D1"])
+        scan(T.GA[:], T.D0[:], T.D1[:], A.add, A.min, ["D0", "D1"], ["GA"])
+        ts(T.GT[:, 0:256], T.GA[:], 2.0, A.is_ge, ["GA"], ["GT1"])
+        if last:
+            ts(Cn[:, 32:256], T.YY[:, 32:256], -1.0, A.max, ["YY"], [cn])
+        for kt in range(2, 8):
+            act(T.GT[:, 256 * kt - 256:256 * kt], T.GA[:], F.Sigmoid, ["GA"], ["GT%d" % kt], scale=200.0, bias=-200.0 * kt - 100.0)
+        act(sm(RL), T.B1[:, 0:32], F.Relu, ["B1t"], ["RL"])
+        so = []
+        for kt, beta in SCANS:
+            a = 256 * kt - 256 + 128 * beta
+            so.append("SO%d%d" % (kt, beta))
+            scan(T.SO[:, a:a + 128], T.GT[:, a:a + 128], half[beta][0][:, 8:136], A.mult, A.add,
+                 ["GT%d" % kt, half[beta][1]], [so[-1]])
+        picks = T.SO[:, 7:1792:8]
+        if last:
+            dma("Y", T.yi[:], T.YI[:], ["YI"], ["yi"])
+            tt(sm(BB), sm(RL), sm(NP), A.add, ["RL", "NP"], ["BB"])
+            tt(T.B6[:, 0:224], picks, T.B7[:, 32:256], A.max, so + zn, ["B6a"])
+            ts(sm(NM), sm(BB), 8.0, A.min, ["BB"], ["NM"])
+            ts(T.GP[:], T.B6[:, 0:224], -1.0, A.mult, ["B6a"], ["GP"], 61440.0, A.add)
+            dma("Y", T.yn[:], sm(NM), ["NM"], ["yn"])
+            tt(T.B6[:, 256:480], T.B6[:, 0:224], T.GP[:], A.min, ["B6a", "GP"], ["B6b"])
+            tt(Cn[:, 32:256], Cn[:, 32:256], T.B6[:, 256:480], A.max, [cn, "B6b"], [cn])
+            dma("A", T.yc[:], Cn[:], [cn, cn + "a"], ["yc"])
+        else:
+            tt(T.B6[:, 256:480], picks, T.B7[:, 32:256], A.max, so + zn, ["B6b"])
+            tt(Cn[:, 32:256], T.EA[:, 32:256], T.B6[:, 256:480], A.min, ["EA", "B6b"], [cn])
+
+    add("Y", None, ["yi", "yn", "yc"], [])
+    add("G", None, [n + str(t) for n in ("sntP", "sntL") for t in range(RO)], [])
+    emit(ops, g, T)

@@ -1,3 +1,4 @@
+from concourse.bass import DstId, RemoteDMATransfer
 from concourse.mybir import AluOpType as A, ActivationFunctionType as F
 
 RO = 3
@@ -18,7 +19,7 @@ def sb(dt, *shape):
 
 
 SCRATCH = {
-    "W": sb(bf, 4112), "S0": sb(bf, 4112), "S2": sb(bf, SW2), "csI": sb(i32, 256), "nsI": sb(i32, 32), "dsI": sb(i32, 32),
+    "W": sb(bf, 4112), "S2": sb(bf, SW2), "csI": sb(i32, 256), "nsI": sb(i32, 32), "dsI": sb(i32, 32),
     "SG": sb(bf, 3584), "OV1": sb(bf, 64, 16), "OV2": sb(bf, 64, 16), "OV3": sb(bf, 64, 16), "OV4": sb(bf, 32, 16),
     "LD": sb(f32, 512), "YI": sb(f32, 512), "IM": sb(f32, 512), "RH": sb(bf, 512),
     "C13": sb(f32, 256), "MX": sb(f32, 256), "XI": sb(i32, 256), "CP": sb(i32, 256),
@@ -41,11 +42,12 @@ for _t in range(RO):
     SCRATCH["GS%d" % _t] = sb(bf, 512)
     SCRATCH["RX%d" % _t] = sb(bf, 16, 32)
     SCRATCH["LP%d" % _t] = sb(f32, 512)
+    SCRATCH["IV%d" % _t] = sb(u16, 32)
 for _t in range(RO + 1):
     SCRATCH["C%d" % _t] = sb(f32, 256)
 
-SEMAPHORES = (["cV", "cA", "cP", "cG"] + ["d%d" % k for k in range(12)]
-              + [n + str(t) for n in ("arrP", "arrL", "sntP", "sntL") for t in range(RO)])
+SEMAPHORES = (["cV", "cA", "cP", "cG", "sntI"] + ["d%d" % k for k in range(12)]
+              + [n + str(t) for n in ("arrP", "arrL", "arrI", "sntP", "sntL") for t in range(RO)])
 
 
 def emit(ops, g, T):
@@ -199,9 +201,8 @@ def rank_program(g, core, T, topo):
     dma("A", T.nsI[:], T.ns[:], [], ["nsI"])
     dma("A", T.csI[:], T.cs[:], [], ["csI"])
     dma("Y", T.W[:, 0:4096], T.wt[:], [], ["Wa"])
-    dma("Y", T.S0[:, 0:4096], T.st[:], [], ["S0a"])
-    add("Y", None, ["S0a"], [])
     dma("Y", T.S2[:, 0:4096], T.st[:], [], ["S2a"])
+    add("Y", None, ["S2a"], [])
     dma("Y", T.S2[:, 4096:8192], T.st[:], [], ["S2b"])
     dma("Y", T.S2[:, 8192:SD2], T.st[:, 0:160], [], ["S2c"])
 
@@ -246,7 +247,6 @@ def rank_program(g, core, T, topo):
     key_const(1)
 
     ms(T.W[:, 4096:4112], 0.0, ["Wb"])
-    ms(T.S0[:, 4096:4112], 1024.0, ["S0b"])
     ms(T.S2[:, SD2:SW2], 1024.0, ["S2d"])
     ms(T.OWN0[:, 0:512], 0.0, ["OWN0.0"])
     ms(T.ONE[:], 1.0, ["ONE"])
@@ -300,19 +300,34 @@ def rank_program(g, core, T, topo):
             act(out[:, 32 * k:32 * k + 32], sm(NP), F.Identity, ["NP"], [w % k], scale=-2 * DEAD * sign,
                 bias=sign * DEAD * (2 * k + 1))
 
+    def target(t):
+        return T.cores[(rank + 1 + t % (N - 1)) % N]
+
     def invert_p():
         for r in range(16):
             mm(T.B7[:, 224:256], T.Z16[:, 15 - r:143 - r], T.SV[:, r:512:16], r == 0, r == 15, ["Z16", "SV"], ["B7i"])
 
+    def invert_a():
+        ts(T.invL[:], T.B7[:, 224:256], -64.0, A.add, ["B7i"], ["invL"])
+        e = topo.engines(core, target(0))
+        part = (e[:len(e) // 2], e[len(e) // 2:3 * len(e) // 4], e[3 * len(e) // 4:])
+        tf = []
+        for t in range(RO):
+            rid, pid = topo.addr(target(t))[:2]
+            tf.append(RemoteDMATransfer(dst_ids=[DstId(rid=rid, pnc=pid)], dma_engine_mask=sum(1 << k for k in part[t]),
+                                        remote_sem=T.sem["arrI%d" % t], src=T.invL[:], dst=T["IV%d" % t][:]))
+        add("G", lambda: g.remote_dma_fused(tf, local_sem=T.sem["sntI"]), ["invL"], ["sntI"], sem="sntI", n=len(e), own=True)
+        for t in range(RO):
+            add("G", None, [], ["IV%d" % t], sem="arrI%d" % t, n=len(part[t]), ext=True)
+
     def invert_b():
-        cp(smi(1), T.B7[:, 224:256], ["B7i"], ["si"])
+        cp(smi(1), T.invL[:], ["invL"], ["si"])
         ts(T.S2K[:], T.IO[:, 32:48], col(c8R), A.add, ["IOc", "c8R"], ["S2K"])
         ts(smi(2), smi(1), 4, A.logical_shift_right, ["si"], ["par"], 1, A.bitwise_and)
-        ts(T.invL[:], smi(1), -64.0, A.add, ["si"], ["invL"])
         ts(sm(YV), smi(2), col(cC1), A.mult, ["par", "cC0", "cC1"], ["YV"], col(cC0), A.add)
         tt(sm(ZV), sm(YV), smi(1), A.add, ["YV", "si"], ["ZV"])
-        cp(T.invP[:, 0:32:2], T.sm[:, 32 * ZV:32 * ZV + 16], ["ZV"], ["invPa"])
-        cp(T.invP[:, 1:32:2], T.sm[:, 32 * ZV + 16:32 * ZV + 32], ["ZV"], ["invPb"])
+        ts(T.invP[:, 0:32:2], T.sm[:, 32 * ZV:32 * ZV + 16], 64.0, A.add, ["ZV"], ["invPa"])
+        ts(T.invP[:, 1:32:2], T.sm[:, 32 * ZV + 16:32 * ZV + 32], 64.0, A.add, ["ZV"], ["invPb"])
 
     for k in range(8):
         ts(T.ZZ[:, 32 * k:32 * k + 32], T.nsI[:], -2 * DEAD, A.mult, ["nsI"], ["ZZ%d" % k], DEAD * (2 * k + 1), A.add)
@@ -328,13 +343,15 @@ def rank_program(g, core, T, topo):
         last = t == RO - 1
         ver = min(t, 1)
         TOP, tb, order = TOPS[ver], BANKS[ver], ORDER[ver].split()
+        if t == 0:
+            order.insert(order.index("c6"), "J")
         fin = int([x for x in order if x[0] == "n"][-1][1])
 
         def ow(b):
             return "OWN%d.%d" % (t, b)
 
-        ts(T.cW[:], C[:, 32:256], 4096.0, A.min, [c], ["cW"])
         ts(T.B6[:, 0:224], C[:, 0:224], 4096.0, A.min, [c, c + "a"], ["B6a"])
+        ts(T.cW[:], C[:, 32:256], 4096.0, A.min, [c], ["cW"])
         if t > 0:
             act(T.B7[:, 0:224], C[:, 32:256], F.Identity, [c], ["B7a"], bias=77.0 * t)
             act(T.RH[:], T.W[:, 0:4112].indirect(T.cW[:, 0:32]), F.Identity, ["Wa", "Wb", "cW"], ["RH"])
@@ -342,9 +359,9 @@ def rank_program(g, core, T, topo):
         ts(T.QI[:], T.PR[:], 5, A.logical_shift_right, ["PR"], ["QI"], 4095, A.bitwise_and)
         if t == 0:
             tt(T.HI[:], T.QI[:], C[:, 32:256], A.add, ["QI", c], ["HI"])
-            ts(T.QI[:], T.HI[:], 0x10FFF, A.bitwise_and, ["HI"], ["QI"])
-            ts(T.hS[:], T.QI[:], 4096.0, A.min, ["QI"], ["hS"])
-            win, wtok = T.S0[:, 0:4112], ["S0a", "S0b"]
+            ts(T.QI[:], T.HI[:], 4095, A.bitwise_and, ["HI"], ["QI"])
+            cp(T.hS[:], T.QI[:], ["QI"], ["hS"])
+            win, wtok = T.S2[:, 0:4096], ["S2a"]
             act_consts()
         else:
             tt(T.HI[:], T.QI[:], T.B7[:, 0:224], A.add, ["QI", "B7a"], ["HI"])
@@ -421,7 +438,7 @@ def rank_program(g, core, T, topo):
             if x[0] in steps:
                 steps[x[0]](int(x[1]))
             else:
-                {"I": invert_p, "S": sum_const, "P": pre_const, "H": heights, "K": keep}[x]()
+                {"I": invert_p, "J": invert_a, "S": sum_const, "P": pre_const, "H": heights, "K": keep}[x]()
         if t == 0:
             act_consts_late()
 
@@ -429,10 +446,12 @@ def rank_program(g, core, T, topo):
         scan(T.MX[:], T.RM[:], T.B0[:, 0:256], A.mult, A.max, ["RM", "B0k"], ["MX"])
         mm(T.B4[:, 256:288], T.SR[:], mx, False, True, ["SR", "MX"], ["B4s"])
         act(sm(THR), mx, F.Relu, ["MX"], ["THR"], scale=-1.0, bias=13968.0)
-        grow_const(t)
         tt(T.XI[:], T.B0[:, 0:256], T.C13[:], A.add, ["B0k", "C13"], ["XI"])
-        tt(T.RD[:], T.B4[:, 256:288], sm(THR), A.is_ge, ["B4s", "THR"], ["RD"])
+        cp(smi(0), mx, ["MX"], ["mi"])
         ts(T.CP[:], T.XI[:], 4, A.logical_shift_right, ["XI"], ["CP"], 0x10FFF, A.bitwise_and)
+        tt(T.RD[:], T.B4[:, 256:288], sm(THR), A.is_ge, ["B4s", "THR"], ["RD"])
+        cp(T.B6[:, 256:512], T.CP[:], ["CP"], ["B6b"])
+        act(T.PB[:, 14:526:2], T.B6[:, 256:512], F.Identity, ["B6b"], ["PBh", "PB14"])
         scan(T.CS[:, 1:33], T.ONE[:], T.RD[:], A.mult, A.add, ["ONE", "RD"], ["CS"])
         mm(T.B7[:, 256:288], T.TRI[:], T.RD[:], False, False, ["TRI", "RD"], ["B7p"])
         mm(T.B7[:, 256:288], T.GB[:], T.CS[:, 0:32], False, True, ["GB", "CS"], ["B7p"])
@@ -442,33 +461,31 @@ def rank_program(g, core, T, topo):
         if t > 0:
             mm(T.B1[:], T.NI[:], OWN[:, 3072:3584], True, False, ["NI", ow(6)], ["B1t"])
             mm(T.B1[:], T.NB[:], T.RH[:], False, True, ["NB", "RH"], ["B1t"])
-        cp(T.B6[:, 256:512], T.CP[:], ["CP"], ["B6b"])
-        act(T.PB[:, 14:526:2], T.B6[:, 256:512], F.Identity, ["B6b"], ["PBh", "PB14"])
-        cp(smi(0), mx, ["MX"], ["mi"])
         ts(smi(3), smi(0), 15, A.bitwise_and, ["mi"], ["A15"])
         tt(T.PB[:, 15:527:2], T.B6[:, 256:512], T.PB[:, 14:526:2], A.subtract, ["B6b", "PBh", "PB14"], ["PBl", "PB15"])
         act(T.PB[:, 30:528:16], sm(NM), F.Identity, ["NM"], ["PB14"])
+        grow_const(t)
         f15 = T.PB[:, 31:528:16]
         tt(f15, T.B7[:, 256:288], smi(3), A.min, ["B7p", "A15"], ["PB15"])
         pb = ["PBh", "PBl", "PB14", "PB15"]
         tr(T.FW[:, 0:512], T.PB[:, 16:528], pb, ["FWa"])
         tr(T.FW[:, 512:1056], T.PB[:, 0:544], pb, ["FWb"])
 
-        dst = T.cores[(rank + 1 + t % (N - 1)) % N]
+        dst = target(t)
         eng = topo.engines(core, dst)
-        eP, eL = (eng[0::2], eng[1::2]) if t == 0 else (eng, eng)
         GS, RX, LP = T["GS%d" % t], T["RX%d" % t], T["LP%d" % t]
         fw = ["FWa", "FWb", "invPa", "invPb"]
         act(GS[:, 0:256], T.FW[:, 0:1056].indirect(T.invP[:, 0:16]), F.Identity, fw, ["GSa%d" % t])
         if t > 0:
             act(OWN[:, 3584:4096], T.B1[:], F.Identity, ["B1t"], [ow(7)], scale=-1.0)
-        cp(GS[:, 256:512], T.FW[:, 0:1056].indirect(T.invP[:, 16:32]), fw, ["GSb%d" % t])
-        send(dst, RX[:], GS[:], eP, "arrP%d" % t, "sntP%d" % t, ["GSa%d" % t, "GSb%d" % t])
         ts(sm(M15), f15, -1.0, A.mult, ["PB15"], ["M15"], 16.0, A.add)
+        cp(GS[:, 256:512], T.FW[:, 0:1056].indirect(T.invP[:, 16:32]), fw, ["GSb%d" % t])
+        send(dst, RX[:], GS[:], eng, "arrP%d" % t, "sntP%d" % t, ["GSa%d" % t, "GSb%d" % t])
         ts(sm(W5), sm(M15), 8.0, A.min, ["M15"], ["W5"], -512.0, A.mult)
         tt(sm(NP), sm(M15), sm(G1), A.min, ["M15", "G1"], ["NP"])
         tt(sm(OFF), sm(W5), sm(S4096), A.add, ["W5", "S4096"], ["OFF"])
         levels(T.ZZ, 1, "ZZ%d")
+        scan(T.SC[:], T.GD[:, 256 * t:256 * t + 256], T.B6[:, 256:512], A.add, A.min, ["GD%d" % t, "B6b"], ["SC"])
         cp(T.OF[:], sm(OFF), ["OFF"], ["OF"])
         ownw, owt = OWN[:, 0:4096].indirect(T.OF[:, 0:32]), ["OF"] + [ow(b) for b in range(8)]
         if t == 0:
@@ -476,17 +493,12 @@ def rank_program(g, core, T, topo):
         else:
             tt(T.LD[:], ownw, T.IM[:], A.subtract, owt + ["IM"], ["LD"])
         act(sm(NPM), sm(NP), F.Identity, ["NP"], ["NPM"], bias=-15.0)
-        if not last:
-            levels(T.B7, -1, "B7z%d")
-        act(LP[:], T.LD[:, 0:512].indirect(T.invL[:, 0:32]), F.Identity, ["LD", "invL"], ["LP%d" % t])
-        if last:
-            levels(T.B7, -1, "B7z%d")
+        levels(T.B7, -1, "B7z%d")
         zn = ["B7z%d" % k for k in range(1, 8)]
-        send(dst, T.YI[:] if last else T["OWN%d" % (t + 1)][:, 0:512], LP[:], eL, "arrL%d" % t, "sntL%d" % t, ["LP%d" % t])
-        add("G", None, [], ["RX%d" % t], sem="arrP%d" % t, n=len(eP), ext=True)
-        add("G", None, [], ["YI" if last else "OWN%d.0" % (t + 1)], sem="arrL%d" % t, n=len(eL), ext=True)
+        send(dst, LP[:], T.LD[:], eng, "arrL%d" % t, "sntL%d" % t, ["LD"])
+        add("G", None, [], ["RX%d" % t], sem="arrP%d" % t, n=len(eng), ext=True)
+        add("G", None, [], ["LP%d" % t], sem="arrL%d" % t, n=len(eng), ext=True)
 
-        scan(T.SC[:], T.GD[:, 256 * t:256 * t + 256], T.B6[:, 256:512], A.add, A.min, ["GD%d" % t, "B6b"], ["SC"])
         tt(T.EI[:], T.SC[:, 0:256].indirect(T.S2K[:, 0:16]), T.ZZ[:], A.max, ["SC", "S2K"] + ZT, ["EI"])
         ts(T.EA[:], T.EI[:], 0x10FFF, A.bitwise_and, ["EI"], ["EA"])
 
@@ -516,6 +528,8 @@ def rank_program(g, core, T, topo):
         for kt in range(2, 8):
             act(T.GT[:, 256 * kt - 256:256 * kt], T.GA[:], F.Sigmoid, ["GA"], ["GT%d" % kt], scale=200.0, bias=-200.0 * kt - 100.0)
         act(sm(RL), T.B1[:, 0:32], F.Relu, ["B1t"], ["RL"])
+        act(T.YI[:] if last else T["OWN%d" % (t + 1)][:, 0:512], LP[:, 0:512].indirect(T["IV%d" % t][:, 0:32]), F.Identity,
+            ["LP%d" % t, "IV%d" % t], ["YI" if last else "OWN%d.0" % (t + 1)])
         so = []
         for kt, beta in SCANS:
             a = 256 * kt - 256 + 128 * beta
@@ -538,5 +552,5 @@ def rank_program(g, core, T, topo):
             tt(Cn[:, 32:256], T.EA[:, 32:256], T.B6[:, 256:480], A.min, ["EA", "B6b"], [cn])
 
     add("Y", None, ["yi", "yn", "yc"], [])
-    add("G", None, [n + str(t) for n in ("sntP", "sntL") for t in range(RO)], [])
+    add("G", None, ["sntI"] + [n + str(t) for n in ("sntP", "sntL") for t in range(RO)], [])
     emit(ops, g, T)

from concourse.bass import DstId, RemoteDMATransfer
from concourse.mybir import AluOpType as A, ActivationFunctionType as F

RO = 3
TOPS = ((4,), (7, 3))
ORDER = ("K S s6 o7 o6 s7 I P t6 s3 s4 o5 t7 t3 o4 c6 o3 s2 c7 o2 u4 c3 t4 t2 s5 c2 s1 o1 c4 n3 t5 c5 n2 t1 c1 n4 n1 H",
         "S P s4 t4 s5 o7 s6 o6 o5 u7 t5 s7 s3 o4 t7 c7 s2 c4 s1 o3 c5 t6 t3 n4 o2 u3 t2 c6 t1 c3 K c2 n3 c1 n2 n1 H")
BANKS = ({6: 1, 7: 2, 3: 3, 4: 5, 2: 1, 5: 2, 1: 3}, {4: 1, 7: 2, 5: 3, 6: 5, 3: 1, 2: 2, 1: 3})
SCANS = ((1, 0), (2, 0), (3, 0), (4, 0), (1, 1), (2, 1), (5, 0), (3, 1), (4, 1), (6, 0), (5, 1), (7, 0), (6, 1), (7, 1))
DEAD = 65536.0
SW2 = 8368
SD2 = 8352

f32, bf, i32, u16 = "float32", "bfloat16", "int32", "uint16"


def sb(dt, *shape):
    return ("sbuf", [128] + list(shape), dt)


SCRATCH = {
    "W": sb(bf, 4112), "S2": sb(bf, SW2), "csI": sb(i32, 256), "nsI": sb(i32, 32), "dsI": sb(i32, 32),
    "SG": sb(bf, 3584), "OV1": sb(bf, 64, 16), "OV2": sb(bf, 64, 16), "OV3": sb(bf, 64, 16), "OV4": sb(bf, 32, 16),
    "LD": sb(f32, 512), "YI": sb(f32, 512), "IM": sb(f32, 512), "RH": sb(bf, 512),
    "C13": sb(f32, 256), "MX": sb(f32, 256), "XI": sb(i32, 256), "CP": sb(i32, 256),
    "PB": sb(bf, 544), "FW": sb(bf, 1056), "RT": sb(bf, 16, 32), "SO": sb(f32, 1792),
    "D0": sb(bf, 256), "D1": sb(bf, 256), "GA": sb(bf, 256), "GT": sb(bf, 1792),
    "PR": sb(i32, 224), "QI": sb(i32, 224), "HI": sb(i32, 224), "cW": sb(u16, 224), "hS": sb(u16, 224),
    "GP": sb(f32, 224), "EI": sb(i32, 256), "EA": sb(i32, 256), "YY": sb(f32, 256), "ZZ": sb(f32, 256), "SC": sb(f32, 256),
    "sm": sb(f32, 16 * 32), "smi": sb(i32, 4 * 32), "OF": sb(u16, 32), "RD": sb(bf, 32), "CS": sb(bf, 48), "ONE": sb(bf, 32),
    "I8": sb(bf, 128), "NI": sb(f32, 128), "NB": sb(bf, 128), "Z1": sb(f32, 144), "ZA": sb(bf, 144), "ZB": sb(bf, 144),
    "Z16": sb(f32, 144), "GB": sb(bf, 128), "TRI": sb(bf, 128), "SR": sb(f32, 128), "SH": sb(f32, 160), "SHM": sb(bf, 4 * 160),
    "NKC": sb(f32, 512), "RM": sb(f32, 256), "DPC": sb(bf, 136), "PC": sb(bf, 32),
    "GI": sb(f32, 256), "GD": sb(f32, 3 * 256), "SI": sb(f32, 512), "SV": sb(f32, 512),
    "pI": sb(i32, 8), "col": sb(f32, 16), "IO": sb(f32, 128),
    "K2S": sb(u16, 16), "S2K": sb(u16, 16), "dsU": sb(u16, 32), "invL": sb(u16, 32), "invP": sb(u16, 32),
}
for _b in range(8):
    SCRATCH["B%d" % _b] = ("psum", [128, 512], f32)
for _t in range(RO):
    SCRATCH["OWN%d" % _t] = sb(f32, 4096)
    SCRATCH["GS%d" % _t] = sb(bf, 512)
    SCRATCH["RX%d" % _t] = sb(bf, 16, 32)
    SCRATCH["LP%d" % _t] = sb(f32, 512)
    SCRATCH["IV%d" % _t] = sb(u16, 32)
for _t in range(RO + 1):
    SCRATCH["C%d" % _t] = sb(f32, 256)

SEMAPHORES = (["cV", "cA", "cP", "cG", "sntI"] + ["d%d" % k for k in range(12)]
              + [n + str(t) for n in ("arrP", "arrL", "arrI", "sntP", "sntL") for t in range(RO)])


def emit(ops, g, T):
    queue = {"V": g.vector, "A": g.scalar, "P": g.tensor, "G": g, "Y": g.sync}
    known = {q: {} for q in queue}
    lastw, readers, bank, count = {}, {}, {}, {}
    waits, snap, ident, needed = [], [], [], set()
    for j, op in enumerate(ops):
        q = op["q"]
        deps = set()
        for tk in op["r"]:
            if tk in lastw:
                deps.add(lastw[tk])
        for tk in op["w"]:
            if tk in lastw:
                deps.add(lastw[tk])
            deps.update(readers.get(tk, []))
        banks = set(tk[:2] for tk in op["r"] + op["w"] if tk[0] == "B" and tk[1].isdigit())
        for b in banks:
            for oq, d in bank.get(b, {}).items():
                if oq != q:
                    deps.add(d)
        wl = []
        for d in sorted(deps, reverse=True):
            key, seq = ident[d]
            if key == "P" and q == "P":
                continue
            if known[q].get(key, -1) >= seq:
                continue
            wl.append(d)
            needed.add(d)
            for k2, s2 in snap[d].items():
                if known[q].get(k2, -1) < s2:
                    known[q][k2] = s2
        waits.append(wl)
        if op["sem"] is None:
            key = q
            seq = count.get(q, 0)
            count[q] = seq + 1
        else:
            key, seq = op["sem"], 0
        ident.append((key, seq))
        s = {} if op["ext"] else dict(known[q])
        s[key] = seq
        snap.append(s)
        if op["fn"] is not None or op["ext"]:
            for tk in op["r"]:
                readers.setdefault(tk, []).append(j)
        for tk in op["w"]:
            lastw[tk] = j
            readers[tk] = []
        for b in banks:
            bank.setdefault(b, {})[q] = j
    value, run = {}, {}
    for j, op in enumerate(ops):
        if op["sem"] is not None:
            value[j] = (op["sem"], op["n"])
        elif j in needed:
            run[op["q"]] = run.get(op["q"], 0) + 1
            value[j] = ("c" + op["q"], run[op["q"]])
    for j, op in enumerate(ops):
        for d in waits[j]:
            queue[op["q"]].wait_ge(T.sem[value[d][0]], value[d][1])
        if op["fn"] is None:
            continue
        ins = op["fn"]()
        if op["own"]:
            continue
        if op["sem"] is not None:
            ins.then_inc(T.sem[op["sem"]], op["n"])
        elif j in needed:
            ins.then_inc(T.sem["c" + op["q"]], 1)


def rank_program(g, core, T, topo):
    rank = T.rank_of(core)
    if rank is None:
        return
    N = len(T.cores)
    ops = []
    V, S, P = g.vector, g.scalar, g.tensor

    def add(q, fn, r, w, sem=None, n=0, ext=False, own=False):
        ops.append({"q": q, "fn": fn, "r": list(r), "w": list(w), "sem": sem, "n": n, "ext": ext, "own": own})

    def tt(out, a, b, op, r, w):
        add("V", lambda: V.tensor_tensor(out, a, b, op), r, w)

    def ts(out, a, s1, op0, r, w, s2=None, op1=None):
        if op1 is None:
            add("V", lambda: V.tensor_scalar(out, a, s1, None, op0), r, w)
        else:
            add("V", lambda: V.tensor_scalar(out, a, s1, s2, op0, op1), r, w)

    def cp(out, a, r, w):
        add("V", lambda: V.tensor_copy(out, a), r, w)

    def ms(ap, v, w):
        add("V", lambda: V.memset(ap, v), [], w)

    def scan(out, d0, d1, op0, op1, r, w):
        add("V", lambda: V.tensor_tensor_scan(out, d0, d1, 0.0, op0, op1), r, w)

    def tr(out, a, r, w):
        add("V", lambda: V.transpose(out, a), r, w)

    def act(out, a, fn, r, w, bias=0.0, scale=1.0):
        add("A", lambda: S.activation(out, a, fn, bias=bias, scale=scale), r, w)

    def mm(out, lhsT, rhs, start, stop, r, w):
        add("P", lambda: P.matmul(out, lhsT, rhs, start, stop), r, w)

    def iota(out, pat, base, cm, w, isint=False):
        if isint:
            add("G", lambda: g.iota(out, pat, base, cm), [], w)
        else:
            add("G", lambda: g.iota(out, pat, base, cm, allow_small_or_imprecise_dtypes=True), [], w)

    def fill(out, n, v, w):
        iota(out, [[0, n]], v, 0, w)

    def sel(out, a, pat, op, fv, base, cm, r, w):
        add("G", lambda: g.affine_select(out, a, pat, op, fv, base, cm), r, w)

    nd = [0]

    def dma(q, out, a, r, w):
        e = g.sync if q == "Y" else g.scalar
        add(q, lambda: e.dma_start(out, a), r, w, sem="d%d" % nd[0], n=16)
        nd[0] += 1

    def send(dst, out, src, e, arr, snt, toks):
        rid, pid = topo.addr(dst)[:2]
        m = sum(1 << k for k in e)
        add("G", lambda: g.remote_dma(out, src, T.sem[arr], T.sem[snt], pid, rid, m), toks, [snt], sem=snt, n=len(e), own=True)

    def sm(k):
        return T.sm[:, 32 * k:32 * k + 32]

    def smi(k):
        return T.smi[:, 32 * k:32 * k + 32]

    def col(k):
        return T.col[:, k:k + 1]

    (THR, NM, G1, M15, NP, W5, OFF, NPM, RL, BB, S4096, YV, ZV, C873) = range(14)
    (cR, cGam, cK2S, c8R, c31, c31b, c31c, cNR, cB0, cB1, cC0, cC1, cT0, cT1) = range(14)
    ZT = ["ZZ%d" % k for k in range(8)]

    dma("A", T.dsI[:], T.ds[:], [], ["dsI"])
    dma("A", T.nsI[:], T.ns[:], [], ["nsI"])
    dma("A", T.csI[:], T.cs[:], [], ["csI"])
    dma("Y", T.W[:, 0:4096], T.wt[:], [], ["Wa"])
    dma("Y", T.S2[:, 0:4096], T.st[:], [], ["S2a"])
    add("Y", None, ["S2a"], [])
    dma("Y", T.S2[:, 4096:8192], T.st[:], [], ["S2b"])
    dma("Y", T.S2[:, 8192:SD2], T.st[:, 0:160], [], ["S2c"])

    def key_const(v):
        iota(T.NKC[:, 256 * v:256 * v + 256], [[0, 32], [1, 8]], -16, 0, ["NKC%d" % v])
        for k in TOPS[v]:
            fill(T.NKC[:, 256 * v + k:256 * v + 256:8], 32, k - 16 - 12416, ["NKC%d" % v])

    iota(T.pI[:, 0:1], [[0, 1]], 0, 1, ["pI0"], True)
    iota(T.SI[:], [[1, 512]], 64, 0, ["SI"])
    iota(T.IO[:, 16:32], [[2, 16]], 0, 0, ["IOb"])
    key_const(0)
    z8 = T.Z1[:, 15:128:16]
    ms(T.Z1[:], 0.0, ["Z1"])
    ms(T.I8[:], 8.0, ["I8"])
    ms(T.NI[:], -1.0, ["NI"])
    ms(z8, 1.0, ["Z1"])
    ms(T.GB[:], -16.0, ["GB"])
    ms(T.SH[:], 1.0, ["SH"])
    sel(T.I8[:], T.I8[:], [[-1, 128]], A.is_equal, 0.0, 0, 1, ["I8"], ["I8"])
    sel(T.NI[:], T.NI[:], [[-1, 128]], A.is_equal, 0.0, 0, 1, ["NI"], ["NI"])
    sel(z8, z8, [[-16, 8]], A.is_ge, 0.0, 0, 1, ["Z1"], ["Z1"])
    iota(T.SR[:], [[0, 8], [1, 16]], 0, 0, ["SR"])
    sel(z8, z8, [[16, 8]], A.is_ge, 0.0, 15, -1, ["Z1"], ["Z1"])
    iota(T.IO[:, 64:96], [[16, 32]], 0, 0, ["IOd"])
    iota(T.IO[:, 32:48], [[1, 8], [128, 2]], 0, 0, ["IOc"])
    sel(T.GB[:], T.GB[:], [[-16, 8], [0, 16]], A.is_ge, 0.0, 0, 1, ["GB"], ["GB"])
    sel(T.SH[:], T.SH[:], [[1, 160]], A.is_equal, 0.0, -16, -1, ["SH"], ["SH"])
    sel(T.GB[:], T.GB[:], [[16, 8], [0, 16]], A.is_ge, 0.0, 15, -1, ["GB"], ["GB"])
    iota(T.GI[:], [[496, 32], [0, 8]], 4096, 0, ["GI"])
    sel(T.TRI[:], T.GB[:], [[1, 128]], A.is_gt, 0.0, 0, -1, ["GB"], ["TRI"])
    fill(T.RM[:], 256, 1, ["RM"])
    sel(T.TRI[:], T.TRI[:], [[1, 128]], A.not_equal, 16384.0, 0, -1, ["TRI"], ["TRI"])
    fill(T.RM[:, 0:256:8], 32, 0, ["RM"])
    fill(T.PB[:], 544, 0, ["PBh", "PBl", "PB14", "PB15"])
    fill(T.DPC[:], 136, 0, ["DPC"])
    fill(T.D0[:], 256, 1, ["D0"])
    fill(T.DPC[:, 14:136:8], 16, -16384, ["DPC"])
    fill(T.D1[:], 256, 1048576, ["D1"])
    fill(T.DPC[:, 15:136:8], 16, 16384, ["DPC"])
    fill(T.D0[:, 0:256:8], 32, 1048576, ["D0"])
    key_const(1)

    ms(T.W[:, 4096:4112], 0.0, ["Wb"])
    ms(T.S2[:, SD2:SW2], 1024.0, ["S2d"])
    ms(T.OWN0[:, 0:512], 0.0, ["OWN0.0"])
    ms(T.ONE[:], 1.0, ["ONE"])
    ms(T.CS[:], 0.0, ["CS"])
    ms(T.PC[:], -1792.0, ["PC"])
    ms(sm(C873), 873.0, ["C873"])
    ts(T.pI[:, 1:2], T.pI[:, 0:1], 15, A.bitwise_and, ["pI0"], ["pI1"])
    ts(T.pI[:, 2:3], T.pI[:, 0:1], 4, A.logical_shift_right, ["pI0"], ["pI2"], 1, A.bitwise_and)
    ts(T.pI[:, 3:4], T.pI[:, 0:1], 7, A.bitwise_and, ["pI0"], ["pI3"])
    ts(T.pI[:, 4:5], T.pI[:, 0:1], 3, A.logical_shift_right, ["pI0"], ["pI4"], 1, A.bitwise_and)
    cp(col(cR), T.pI[:, 1:2], ["pI1"], ["cR"])
    ts(col(cT0), T.pI[:, 3:4], 32.0, A.mult, ["pI3"], ["cT0"])
    cp(col(cGam), T.pI[:, 2:3], ["pI2"], ["cGam"])
    cp(T.dsU[:], T.dsI[:], ["dsI"], ["dsU"])
    add("A", lambda: S.activation(T.SV[:, 0:512].indirect(T.dsU[:, 0:32]), T.SI[:], F.Silu), ["dsU", "SI"], ["SV"])
    tt(col(cK2S), col(cT0), T.pI[:, 4:5], A.add, ["cT0", "pI4"], ["cK2S"])

    def act_consts():
        act(T.Z16[:], T.Z1[:], F.Identity, ["Z1"], ["Z16"], scale=0.0625)
        act(T.ZA[:], T.Z1[:], F.Identity, ["Z1"], ["ZA"], scale=1552.0)
        act(T.ZB[:], T.Z1[:], F.Identity, ["Z1"], ["ZB"], scale=776.0)
        act(T.NB[:], T.NI[:], F.Identity, ["NI"], ["NB"])
        act(col(c8R), col(cR), F.Identity, ["cR"], ["c8R"], scale=8.0)
        for t in range(RO):
            act(col(c31 + t), col(cR), F.Identity, ["cR"], ["c31%d" % t], scale=31.0, bias=997.0 * t)
        act(col(cNR), col(cR), F.Identity, ["cR"], ["cNR"], scale=-1.0)
        act(col(cB0), col(cGam), F.Identity, ["cGam"], ["cB0"], scale=-400.0, bias=-100.0)
        act(col(cB1), col(cGam), F.Identity, ["cGam"], ["cB1"], scale=400.0, bias=-500.0)
        act(col(cC0), col(cGam), F.Identity, ["cGam"], ["cC0"], scale=528.0, bias=-64.0)
        act(col(cC1), col(cGam), F.Identity, ["cGam"], ["cC1"], scale=-1056.0, bias=528.0)
        act(col(cT1), col(cR), F.Identity, ["cR"], ["cT1"], bias=4096.0)
        act(T.SR[:], T.SR[:], F.Abs, ["SR", "cNR"], ["SR"], bias=col(cNR))
        act(sm(S4096), T.IO[:, 64:96], F.Identity, ["IOd", "cT1"], ["S4096"], bias=col(cT1))
        act(T.SR[:], T.SR[:], F.Relu, ["SR"], ["SR"], scale=-1.0 / 128, bias=1.0 / 128)

    def act_consts_late():
        for k, nm in enumerate(("cB0", "cB1")):
            act(T.SHM[:, 160 * k:160 * k + 160], T.SH[:], F.Sigmoid, ["SH", nm], ["SHM%d" % k], scale=200.0, bias=col(cB0 + k))
        act(T.SHM[:, 320:640], T.SHM[:, 0:320], F.Identity, ["SHM0", "SHM1"], ["SHM2", "SHM3"], scale=-1.0)

    def grow_const(t):
        act(T.GD[:, 256 * t:256 * t + 256], T.GI[:], F.Identity, ["GI", "c31%d" % t], ["GD%d" % t], bias=col(c31 + t))

    def shm(beta, gam, neg):
        a = 160 * (beta + 2 * neg) + 16 - 16 * (gam - beta)
        return T.SHM[:, a:a + 128]
    SHT = ["SHM%d" % k for k in range(4)] + ["RT"]

    def levels(out, sign, w):
        for k in range(1, 8):
            act(out[:, 32 * k:32 * k + 32], sm(NP), F.Identity, ["NP"], [w % k], scale=-2 * DEAD * sign,
                bias=sign * DEAD * (2 * k + 1))

    def target(t):
        return T.cores[(rank + 1 + t % (N - 1)) % N]

    def invert_p():
        for r in range(16):
            mm(T.B7[:, 224:256], T.Z16[:, 15 - r:143 - r], T.SV[:, r:512:16], r == 0, r == 15, ["Z16", "SV"], ["B7i"])

    def invert_a():
        ts(T.invL[:], T.B7[:, 224:256], -64.0, A.add, ["B7i"], ["invL"])
        e = topo.engines(core, target(0))
        part = (e[:len(e) // 2], e[len(e) // 2:3 * len(e) // 4], e[3 * len(e) // 4:])
        tf = []
        for t in range(RO):
            rid, pid = topo.addr(target(t))[:2]
            tf.append(RemoteDMATransfer(dst_ids=[DstId(rid=rid, pnc=pid)], dma_engine_mask=sum(1 << k for k in part[t]),
                                        remote_sem=T.sem["arrI%d" % t], src=T.invL[:], dst=T["IV%d" % t][:]))
        add("G", lambda: g.remote_dma_fused(tf, local_sem=T.sem["sntI"]), ["invL"], ["sntI"], sem="sntI", n=len(e), own=True)
        for t in range(RO):
            add("G", None, [], ["IV%d" % t], sem="arrI%d" % t, n=len(part[t]), ext=True)

    def invert_b():
        cp(smi(1), T.invL[:], ["invL"], ["si"])
        ts(T.S2K[:], T.IO[:, 32:48], col(c8R), A.add, ["IOc", "c8R"], ["S2K"])
        ts(smi(2), smi(1), 4, A.logical_shift_right, ["si"], ["par"], 1, A.bitwise_and)
        ts(sm(YV), smi(2), col(cC1), A.mult, ["par", "cC0", "cC1"], ["YV"], col(cC0), A.add)
        tt(sm(ZV), sm(YV), smi(1), A.add, ["YV", "si"], ["ZV"])
        ts(T.invP[:, 0:32:2], T.sm[:, 32 * ZV:32 * ZV + 16], 64.0, A.add, ["ZV"], ["invPa"])
        ts(T.invP[:, 1:32:2], T.sm[:, 32 * ZV + 16:32 * ZV + 32], 64.0, A.add, ["ZV"], ["invPb"])

    for k in range(8):
        ts(T.ZZ[:, 32 * k:32 * k + 32], T.nsI[:], -2 * DEAD, A.mult, ["nsI"], ["ZZ%d" % k], DEAD * (2 * k + 1), A.add)
    ts(sm(NM), T.nsI[:], -16.0, A.add, ["nsI"], ["NM"])
    tt(T.YY[:], T.ZZ[:], T.csI[:], A.max, ZT + ["csI"], ["YY"])
    ts(sm(G1), T.nsI[:], 1.0, A.add, ["nsI"], ["G1"], 8.0, A.min)
    ts(T.C0[:], T.YY[:], DEAD, A.min, ["YY"], ["C0"])
    ts(T.K2S[:], T.IO[:, 16:32], col(cK2S), A.add, ["IOb", "cK2S"], ["K2S"])

    for t in range(RO):
        C, Cn, OWN = T["C%d" % t], T["C%d" % (t + 1)], T["OWN%d" % t]
        c, cn = "C%d" % t, "C%d" % (t + 1)
        last = t == RO - 1
        ver = min(t, 1)
        TOP, tb, order = TOPS[ver], BANKS[ver], ORDER[ver].split()
        if t == 0:
            order.insert(order.index("c6"), "J")
        fin = int([x for x in order if x[0] == "n"][-1][1])

        def ow(b):
            return "OWN%d.%d" % (t, b)

        ts(T.B6[:, 0:224], C[:, 0:224], 4096.0, A.min, [c, c + "a"], ["B6a"])
        ts(T.cW[:], C[:, 32:256], 4096.0, A.min, [c], ["cW"])
        if t > 0:
            act(T.B7[:, 0:224], C[:, 32:256], F.Identity, [c], ["B7a"], bias=77.0 * t)
            act(T.RH[:], T.W[:, 0:4112].indirect(T.cW[:, 0:32]), F.Identity, ["Wa", "Wb", "cW"], ["RH"])
        tt(T.PR[:], C[:, 32:256], T.B6[:, 0:224], A.mult, [c, "B6a"], ["PR"])
        ts(T.QI[:], T.PR[:], 5, A.logical_shift_right, ["PR"], ["QI"], 4095, A.bitwise_and)
        if t == 0:
            tt(T.HI[:], T.QI[:], C[:, 32:256], A.add, ["QI", c], ["HI"])
            ts(T.QI[:], T.HI[:], 4095, A.bitwise_and, ["HI"], ["QI"])
            cp(T.hS[:], T.QI[:], ["QI"], ["hS"])
            win, wtok = T.S2[:, 0:4096], ["S2a"]
            act_consts()
        else:
            tt(T.HI[:], T.QI[:], T.B7[:, 0:224], A.add, ["QI", "B7a"], ["HI"])
            ts(T.hS[:], T.HI[:], float(SD2), A.min, ["HI"], ["hS"])
            win, wtok = T.S2[:, 0:SW2], ["S2a", "S2b", "S2c", "S2d"]
        mm(T.B0[:, 0:256], T.NI[:], T.NKC[:, 256 * ver:256 * ver + 256], True, False, ["NI", "NKC%d" % ver], ["B0k"])

        begun = set()

        def o(k):
            b = 8 - k
            tt(OWN[:, 512 * b:512 * b + 512], T.W[:, 0:4112].indirect(T.cW[:, 32 * k - 32:32 * k]),
               OWN[:, 512 * b - 512:512 * b], A.add, ["Wa", "Wb", "cW", ow(b - 1)], [ow(b)])

        def sg(k):
            act(T.SG[:, 512 * k - 512:512 * k], win.indirect(T.hS[:, 32 * k - 32:32 * k]), F.Identity,
                wtok + ["hS"], ["SG%d" % k])

        def tm(k):
            b = tb[k]
            apart = k == 1 and t > 0
            mm(T["B%d" % b][:], T.I8[:], T.SG[:, 512 * k - 512:512 * k], k not in begun,
               (k in begun or k not in TOP) and not apart, ["I8", "SG%d" % k], ["B%dt" % b])
            if apart:
                mm(T["B%d" % b][:], T.NB[:], T.RH[:], False, True, ["NB", "RH"], ["B%dt" % b])
            begun.add(k)

        def to(k):
            b = tb[k]
            mm(T["B%d" % b][:], T.NI[:], OWN[:, 512 * (8 - k):512 * (9 - k)], k not in begun, k in begun,
               ["NI", ow(8 - k)], ["B%dt" % b])
            begun.add(k)

        def cmp(k):
            b = tb[k]
            out = T.OV4[:] if k == 4 else T["OV%d" % (k % 4)][:, k // 4:64:2, :]
            if k in TOP:
                act(out, T["B%d" % b][:], F.Sign, ["B%dt" % b], ["OV%d" % k], scale=-1.0, bias=-0.5)
            else:
                x = 6 if k == 1 and t > 0 else 8 - k
                tt(out, OWN[:, 512 * x:512 * x + 512], T["B%d" % b][:], A.is_gt, [ow(x), "B%dt" % b], ["OV%d" % k])

        def cnt(k):
            z, zt = (T.ZB, "ZB") if k in TOP else (T.ZA, "ZA")
            for r in range(16):
                if k == 4:
                    mm(T.B0[:, 4:256:8], z[:, 15 - r:143 - r], T.OV4[:, :, r], False, k == fin and r == 15, [zt, "OV4"], ["B0k"])
                else:
                    mm(T.B0[:, k:256:4], z[:, 15 - r:143 - r], T["OV%d" % k][:, :, r], False, k == fin and r == 15,
                       [zt, "OV%d" % k, "OV%d" % (k + 4)], ["B0k"])

        def heights():
            if t > 0:
                tt(sm(BB), sm(RL), sm(NP), A.add, ["RL", "NP"], ["BB"])
                ts(sm(NM), sm(BB), 8.0, A.min, ["BB"], ["NM"], -16.0, A.add)
                ts(sm(G1), sm(BB), 1.0, A.add, ["BB"], ["G1"], 8.0, A.min)
            else:
                invert_b()

        def sum_const():
            mm(T.B4[:, 256:288], T.NI[:], sm(C873), True, False, ["NI", "C873"], ["B4s"])

        def pre_const():
            mm(T.B7[:, 256:288], T.I8[:], T.PC[:], True, False, ["I8", "PC"], ["B7p"])

        def keep():
            act(T.C13[:], C[:, 0:256].indirect(T.K2S[:, 0:16]), F.Identity, [c, c + "a", "K2S"], ["C13"], scale=208.0,
                bias=16.0 * t - 1.0)
            if t > 0:
                act(T.IM[:], OWN[:, 0:512], F.Identity, [ow(0)], ["IM"])

        steps = {"o": o, "s": sg, "t": tm, "u": to, "c": cmp, "n": cnt}
        for x in order:
            if x[0] in steps:
                steps[x[0]](int(x[1]))
            else:
                {"I": invert_p, "J": invert_a, "S": sum_const, "P": pre_const, "H": heights, "K": keep}[x]()
        if t == 0:
            act_consts_late()

        mx = T.MX[:, 7:256:8]
        scan(T.MX[:], T.RM[:], T.B0[:, 0:256], A.mult, A.max, ["RM", "B0k"], ["MX"])
        mm(T.B4[:, 256:288], T.SR[:], mx, False, True, ["SR", "MX"], ["B4s"])
        act(sm(THR), mx, F.Relu, ["MX"], ["THR"], scale=-1.0, bias=13968.0)
        tt(T.XI[:], T.B0[:, 0:256], T.C13[:], A.add, ["B0k", "C13"], ["XI"])
        cp(smi(0), mx, ["MX"], ["mi"])
        ts(T.CP[:], T.XI[:], 4, A.logical_shift_right, ["XI"], ["CP"], 0x10FFF, A.bitwise_and)
        tt(T.RD[:], T.B4[:, 256:288], sm(THR), A.is_ge, ["B4s", "THR"], ["RD"])
        cp(T.B6[:, 256:512], T.CP[:], ["CP"], ["B6b"])
        act(T.PB[:, 14:526:2], T.B6[:, 256:512], F.Identity, ["B6b"], ["PBh", "PB14"])
        scan(T.CS[:, 1:33], T.ONE[:], T.RD[:], A.mult, A.add, ["ONE", "RD"], ["CS"])
        mm(T.B7[:, 256:288], T.TRI[:], T.RD[:], False, False, ["TRI", "RD"], ["B7p"])
        mm(T.B7[:, 256:288], T.GB[:], T.CS[:, 0:32], False, True, ["GB", "CS"], ["B7p"])
        half = ((T.B4, "B4d"), (T.B3, "B3t"))
        for bk, tok in half:
            mm(bk[:, 0:136], T.I8[:], T.DPC[:], True, False, ["I8", "DPC"], [tok])
        if t > 0:
            mm(T.B1[:], T.NI[:], OWN[:, 3072:3584], True, False, ["NI", ow(6)], ["B1t"])
            mm(T.B1[:], T.NB[:], T.RH[:], False, True, ["NB", "RH"], ["B1t"])
        ts(smi(3), smi(0), 15, A.bitwise_and, ["mi"], ["A15"])
        tt(T.PB[:, 15:527:2], T.B6[:, 256:512], T.PB[:, 14:526:2], A.subtract, ["B6b", "PBh", "PB14"], ["PBl", "PB15"])
        act(T.PB[:, 30:528:16], sm(NM), F.Identity, ["NM"], ["PB14"])
        grow_const(t)
        f15 = T.PB[:, 31:528:16]
        tt(f15, T.B7[:, 256:288], smi(3), A.min, ["B7p", "A15"], ["PB15"])
        pb = ["PBh", "PBl", "PB14", "PB15"]
        tr(T.FW[:, 0:512], T.PB[:, 16:528], pb, ["FWa"])
        tr(T.FW[:, 512:1056], T.PB[:, 0:544], pb, ["FWb"])

        dst = target(t)
        eng = topo.engines(core, dst)
        GS, RX, LP = T["GS%d" % t], T["RX%d" % t], T["LP%d" % t]
        fw = ["FWa", "FWb", "invPa", "invPb"]
        act(GS[:, 0:256], T.FW[:, 0:1056].indirect(T.invP[:, 0:16]), F.Identity, fw, ["GSa%d" % t])
        if t > 0:
            act(OWN[:, 3584:4096], T.B1[:], F.Identity, ["B1t"], [ow(7)], scale=-1.0)
        ts(sm(M15), f15, -1.0, A.mult, ["PB15"], ["M15"], 16.0, A.add)
        cp(GS[:, 256:512], T.FW[:, 0:1056].indirect(T.invP[:, 16:32]), fw, ["GSb%d" % t])
        send(dst, RX[:], GS[:], eng, "arrP%d" % t, "sntP%d" % t, ["GSa%d" % t, "GSb%d" % t])
        ts(sm(W5), sm(M15), 8.0, A.min, ["M15"], ["W5"], -512.0, A.mult)
        tt(sm(NP), sm(M15), sm(G1), A.min, ["M15", "G1"], ["NP"])
        tt(sm(OFF), sm(W5), sm(S4096), A.add, ["W5", "S4096"], ["OFF"])
        levels(T.ZZ, 1, "ZZ%d")
        scan(T.SC[:], T.GD[:, 256 * t:256 * t + 256], T.B6[:, 256:512], A.add, A.min, ["GD%d" % t, "B6b"], ["SC"])
        cp(T.OF[:], sm(OFF), ["OFF"], ["OF"])
        ownw, owt = OWN[:, 0:4096].indirect(T.OF[:, 0:32]), ["OF"] + [ow(b) for b in range(8)]
        if t == 0:
            cp(T.LD[:], ownw, owt, ["LD"])
        else:
            tt(T.LD[:], ownw, T.IM[:], A.subtract, owt + ["IM"], ["LD"])
        act(sm(NPM), sm(NP), F.Identity, ["NP"], ["NPM"], bias=-15.0)
        levels(T.B7, -1, "B7z%d")
        zn = ["B7z%d" % k for k in range(1, 8)]
        send(dst, LP[:], T.LD[:], eng, "arrL%d" % t, "sntL%d" % t, ["LD"])
        add("G", None, [], ["RX%d" % t], sem="arrP%d" % t, n=len(eng), ext=True)
        add("G", None, [], ["LP%d" % t], sem="arrL%d" % t, n=len(eng), ext=True)

        tt(T.EI[:], T.SC[:, 0:256].indirect(T.S2K[:, 0:16]), T.ZZ[:], A.max, ["SC", "S2K"] + ZT, ["EI"])
        ts(T.EA[:], T.EI[:], 0x10FFF, A.bitwise_and, ["EI"], ["EA"])

        tr(T.RT[:], RX[:], ["RX%d" % t], ["RT"])
        cp(Cn[:, 0:32], T.EA[:, 0:32], ["EA"], [cn + "a"])
        if last:
            tt(T.YY[:, 32:256], T.EA[:, 32:256], T.B7[:, 32:256], A.min, ["EA"] + zn, ["YY"])
        for beta in range(2):
            for gam in range(2):
                mm(T.B5[:, 16 * beta:16 * beta + 16], shm(beta, gam, 0), T.RT[:, :, 16 * gam + 15], gam == 0, gam == 1, SHT, ["B5t"])
        for beta, (bk, tok) in enumerate(half):
            for gam in range(2):
                for h in range(2):
                    a = 16 * gam + h
                    mm(bk[:, 8:136], shm(beta, gam, 0), T.RT[:, :, a:16 * gam + 16:2], False, False, SHT, [tok])
                    mm(bk[:, 7:135], shm(beta, gam, 1), T.RT[:, :, a:16 * gam + 16:2], False, False, SHT, [tok])
                    mm(bk[:, 7:135:8], shm(beta, gam, 0), T.RT[:, :, a], False, gam == 1 and h == 1, SHT, [tok])
        for beta in range(2):
            for x in range(4):
                gam, fld = x // 2, 14 + x % 2
                mm(T.B1[:, 16 * beta:16 * beta + 16], shm(beta, gam, 0), T.RT[:, :, 16 * gam + fld], x == 0, x == 3, SHT, ["B1t"])
        tt(T.D1[:, 0:256:8], T.B5[:, 0:32], sm(NPM), A.add, ["B5t", "NPM"], ["D1"])
        scan(T.GA[:], T.D0[:], T.D1[:], A.add, A.min, ["D0", "D1"], ["GA"])
        ts(T.GT[:, 0:256], T.GA[:], 2.0, A.is_ge, ["GA"], ["GT1"])
        if last:
            ts(Cn[:, 32:256], T.YY[:, 32:256], -1.0, A.max, ["YY"], [cn])
        for kt in range(2, 8):
            act(T.GT[:, 256 * kt - 256:256 * kt], T.GA[:], F.Sigmoid, ["GA"], ["GT%d" % kt], scale=200.0, bias=-200.0 * kt - 100.0)
        act(sm(RL), T.B1[:, 0:32], F.Relu, ["B1t"], ["RL"])
        act(T.YI[:] if last else T["OWN%d" % (t + 1)][:, 0:512], LP[:, 0:512].indirect(T["IV%d" % t][:, 0:32]), F.Identity,
            ["LP%d" % t, "IV%d" % t], ["YI" if last else "OWN%d.0" % (t + 1)])
        so = []
        for kt, beta in SCANS:
            a = 256 * kt - 256 + 128 * beta
            so.append("SO%d%d" % (kt, beta))
            scan(T.SO[:, a:a + 128], T.GT[:, a:a + 128], half[beta][0][:, 8:136], A.mult, A.add,
                 ["GT%d" % kt, half[beta][1]], [so[-1]])
        picks = T.SO[:, 7:1792:8]
        if last:
            dma("Y", T.yi[:], T.YI[:], ["YI"], ["yi"])
            tt(sm(BB), sm(RL), sm(NP), A.add, ["RL", "NP"], ["BB"])
            tt(T.B6[:, 0:224], picks, T.B7[:, 32:256], A.max, so + zn, ["B6a"])
            ts(sm(NM), sm(BB), 8.0, A.min, ["BB"], ["NM"])
            ts(T.GP[:], T.B6[:, 0:224], -1.0, A.mult, ["B6a"], ["GP"], 61440.0, A.add)
            dma("Y", T.yn[:], sm(NM), ["NM"], ["yn"])
            tt(T.B6[:, 256:480], T.B6[:, 0:224], T.GP[:], A.min, ["B6a", "GP"], ["B6b"])
            tt(Cn[:, 32:256], Cn[:, 32:256], T.B6[:, 256:480], A.max, [cn, "B6b"], [cn])
            dma("A", T.yc[:], Cn[:], [cn, cn + "a"], ["yc"])
        else:
            tt(T.B6[:, 256:480], picks, T.B7[:, 32:256], A.max, so + zn, ["B6b"])
            tt(Cn[:, 32:256], T.EA[:, 32:256], T.B6[:, 256:480], A.min, ["EA", "B6b"], [cn])

    add("Y", None, ["yi", "yn", "yc"], [])
    add("G", None, ["sntI"] + [n + str(t) for n in ("sntP", "sntL") for t in range(RO)], [])
    emit(ops, g, T)
